import numpy as np, ml_dtypes
CORES = [25,29,65,69,153,157,193,197]
N = 8
BF = ml_dtypes.bfloat16
def gentries(a):
    return np.ascontiguousarray(a.reshape(8, 16, -1).transpose(0, 2, 1)).reshape(8, -1)
def gtable(e):
    e = np.asarray(e); return np.ascontiguousarray(e.reshape(8, -1, 16).transpose(0, 2, 1)).reshape(128, -1).astype(np.int32)
V, RO, VO, GS = 1536, 2, 8, 1
def mix(rng, p):
    return [p[i] for i in rng.permutation(len(p))]
def invol(rng, n):
    o = rng.permutation(V); t = np.arange(V); t[o[n::2]] = o[n + 1::2]; t[o[n + 1::2]] = o[n::2]
    return t
def sew(parts, line):
    t = np.arange(V); s = np.arange(V); at = 0
    for n, kind in parts:
        w = line[at:at + n]; at += n
        if n == 1: continue
        two = (t, s) if kind == 1 else (s, t)
        for q in (0, 1):
            e = w[q:]; m = len(e) // 2 * 2; a = e[0:m:2]; b = e[1:m:2]
            two[q][a] = b; two[q][b] = a
        if kind == 2: t[w[0]] = w[n - 1]; t[w[n - 1]] = w[0]
    return t, s
def tie(rng, s, goal, straight):
    v = np.arange(V); u = np.empty(V, np.int64); a = v[s > v]; z = v[goal > v]
    u[rng.permutation(v[s == v])] = v[goal == v]
    if straight: z = goal[z]
    else: a = rng.permutation(a); z = np.where(rng.random(len(z)) < 0.5, z, goal[z])
    u[a] = z; u[s[a]] = goal[z]
    return u
def grow(rng, parts, lines, straight=False):
    b = [sew(parts[r], lines[r]) for r in range(N)]; t = np.stack([y[0] for y in b])
    return t, np.stack([tie(rng, b[r][1], t[(r + 1) % N], straight) for r in range(N)])
def cut(rng, n, top, ring):
    out = []; left = V
    for i in range(n // 2):
        if rng.random() < 0.5: z = 2 * rng.integers(0, top // 2, 2) + 1; y = rng.integers(0, 2, 2)
        else: z = 2 * rng.integers(1, top // 2 + 1, 2); y = (0, 1)
        out += [(int(z[0]), int(y[0])), (int(z[1]), int(y[1]))]; left -= int(z[0] + z[1])
    while left > 0:
        m = min(left, 2 * int(rng.integers(1, ring + 1))); out.append((m, 2)); left -= m
    return mix(rng, out)
CUTS = ((64, 16, 10), (128, 8, 6), (16, 64, 40), (4, 256, 150))
def base(rng):
    t = np.empty((N, 8, V), np.int64); u = np.empty((N, 8, V), np.int64); o = rng.permutation(8)
    for q in range(8):
        g = o[q]
        if q < 4:
            for r in range(N):
                n = int(rng.choice(np.array([0, 2]))) if q == 0 else 2 * int(rng.choice(np.array([0, 1, V // 64, V // 32, V // 16, V // 8, V // 4])))
                t[r, g] = invol(rng, n); u[r, g] = rng.permutation(V)
        else:
            n, top, ring = CUTS[q - 4]
            t[:, g], u[:, g] = grow(rng, [cut(rng, n, top, ring) for r in range(N)], [rng.permutation(V) for r in range(N)])
    return t, u
def hang(rng):
    n = np.array([VO, VO - 1, 16, 0, VO, VO - 1, 15, VO + 1])[(np.arange(8)[None, :] + np.arange(N)[:, None] + rng.integers(0, 8)) % 8][:, :, None, None]
    ok = np.argsort(rng.random((N, 8, 16, 1)), axis=2) < n
    th = rng.choice(np.array([0, 1, 7, 100, 253, 254]), (N, 8, 16, 1)); gap = th + 1 - ok.astype(np.int64)
    low = np.floor(rng.random((N, 8, 16, 1)) * (256 - gap)).astype(np.int64); share = rng.choice(np.array([0.004, 0.03, 0.2, 0.5]), (N, 8, 1, 1))
    hi = (rng.random((N, 8, 1, V)) < share) & (rng.random((N, 8, 16, V)) < 0.75)
    return low + gap * hi, th
def pack(t, u, x, th):
    return {"t0": np.stack([gtable(a) for a in t]), "u0": np.stack([gtable(a) for a in u]),
            "x": np.ascontiguousarray(x.reshape(N, 128, V)).astype(np.float32).astype(BF), "th": np.ascontiguousarray(th.reshape(N, 128, 1)).astype(np.int32)}
def setup_inputs(rng):
    t, u = base(rng)
    th = rng.integers(8, 120, (N, 8, 16, 1)); low = np.floor(rng.random((N, 8, 16, 1)) * (256 - th)).astype(np.int64)
    x = low + np.floor(rng.random((N, 8, 16, V)) * (th + 1)).astype(np.int64)
    share = rng.choice(np.array([0.004, 0.015, 0.04, 0.12]), (N, 8, 1, 1))
    m = (rng.random((N, 8, 1, V)) < share) & (rng.random((N, 8, 16, V)) < rng.random((N, 8, 1, V)))
    return pack(t, u, np.where(m, rng.integers(0, 256, m.shape), x), th)
def setup_inputs_spread(rng):
    t, u = base(rng)
    th = np.floor(np.exp2(8 * rng.random((N, 8, 16, 1)))).astype(np.int64) - (rng.random((N, 8, 16, 1)) < 0.25)
    e = rng.choice(np.array([1.0, 3.0, 8.0]), (N, 8, 1, 1))
    x = np.floor(np.exp2(8 * rng.random((N, 8, 1, V)) ** e) * rng.random((N, 8, 16, V))).astype(np.int64)
    return pack(t, u, x, th)
def setup_inputs_ends(rng):
    zig = np.empty(V, np.int64); zig[0::2] = np.arange(V // 2); zig[1::2] = V - 1 - np.arange(V // 2)
    t = np.empty((N, 8, V), np.int64); u = np.empty((N, 8, V), np.int64)
    for g in range(8):
        if g < 3: lines = [np.roll(zig, 2 * int(rng.integers(0, V // 2))) for r in range(N)]
        elif g < 6: lines = [zig.reshape(-1, 16)[rng.permutation(V // 16)].reshape(-1) for r in range(N)]
        else: lines = [np.arange(V)[::(1, -1)[(r + g) % 2]] for r in range(N)]
        if g == 0: parts = [[(V, r % 2)] for r in range(N)]
        elif g == 1: parts = [[(V - 1, int(rng.integers(0, 2))), (1, 0)] for r in range(N)]
        elif g == 2: parts = [[(V, 2)] for r in range(N)]
        else: parts = [cut(rng, *CUTS[(2, 0, 3, 1, 0)[g - 3]]) for r in range(N)]
        t[:, g], u[:, g] = grow(rng, parts, lines, g % 2 == 1)
    n = np.stack([rng.permutation(np.array([VO, VO - 1, VO - 2, VO - 1, VO - 1, 0, 16, 15])) for r in range(N)])[:, :, None, None]
    all_ = np.argsort(rng.random((N, 8, 16, 1)), axis=2) < n; th = 255 * all_.astype(np.int64)
    e = rng.integers(0, 2, (N, 8, 16, 1)); share = rng.choice(np.array([0.003, 0.02, 0.06]), (N, 8, 1, 1))
    m = (rng.random((N, 8, 1, V)) < share) & (rng.random((N, 8, 16, V)) < rng.random((N, 8, 1, V)))
    m[:, 1::2, :, V - 1] = True; m[:, 0::2, :, 0] = True
    m = np.where(all_, rng.random(m.shape) < 0.5, m)
    return pack(t, u, 255 * (e ^ m.astype(np.int64)), th)
def setup_inputs_corners(rng):
    t = np.empty((N, 8, V), np.int64); u = np.empty((N, 8, V), np.int64); o = rng.permutation(8)
    for q in range(8):
        g = o[q]; lines = [rng.permutation(V) for r in range(N)]
        if q == 0: parts = [[(V, r % 2)] for r in range(N)]
        elif q == 1:
            parts = [[(V - 1, int(rng.integers(0, 2))), (1, 0)] for r in range(N)]; lines = [np.append(rng.permutation(V - 1), V - 1) for r in range(N)]
        elif q == 2: parts = [[(V, 2)] for r in range(N)]
        elif q == 3: parts = [[(V - 2, 2), (2, 2)] for r in range(N)]
        elif q == 4:
            m = V // 6 // 2 * 2; left = V - 4 * (V // 8) - 3 * m
            p = [(2, 0)] * (V // 8) + [(2, 1)] * (V // 8) + [(3, 0)] * (m // 2) + [(3, 1)] * (m // 2) + ([(left, 2)] if left else [])
            parts = [mix(rng, p) for r in range(N)]
        elif q == 5: parts = [mix(rng, [(4, 2), (8, 2), (4, 2)] * (V // 16)) for r in range(N)]
        elif q == 6:
            z = int(rng.integers(0, N))
            for r in range(N): t[r, g] = invol(rng, V if r == z else 2 * int(rng.choice(np.array([0, 1, V // 16, V // 4])))); u[r, g] = rng.permutation(V)
            continue
        else: parts = [cut(rng, *CUTS[0]) for r in range(N)]
        t[:, g], u[:, g] = grow(rng, parts, lines)
    x, th = hang(rng)
    return pack(t, u, x, th)
def setup_inputs_lone(rng):
    t = np.empty((N, 8, V), np.int64); u = np.empty((N, 8, V), np.int64); o = rng.permutation(8)
    pairs = [(2, 0)] * (V // 8) + [(2, 1)] * (V // 8) + [(4, 2)] * (V // 8)
    few = [(3, 0)] * (V // 128) + [(3, 1)] * (V // 128) + [(2, 0)] * (V // 64) + [(2, 1)] * (V // 64) + [(4, 2)] * (V // 128)
    m = 10 * (V // 128) + 4 * (V // 64); still = [(2, 2)] * (V // 8) + [(1, 0)] * (V - m - 2 * (V // 8))
    for q in range(8):
        g = o[q]; lines = [rng.permutation(V) for r in range(N)]
        if q < 2: parts = [[(V, r % 2)] for r in range(N)]
        elif q == 2: parts = [[(V - 16, r % 2), (16, 2)] for r in range(N)]
        elif q < 5:
            parts = [mix(rng, pairs) for r in range(N)]
            if q == 4: lines = [np.arange(V)[::(1, -1)[r % 2]] for r in range(N)]
        elif q == 5:
            parts = [still + mix(rng, few) for r in range(N)]; lines = [np.concatenate([rng.permutation(V - m), V - m + rng.permutation(m)]) for r in range(N)]
        elif q == 6:
            parts = [[(1, 0)] * (V - 2) + [(2, r % 2)] for r in range(N)]; lines = [np.append(rng.permutation(V - 2), [V - 2, V - 1]) for r in range(N)]
        else: parts = [mix(rng, still + few) for r in range(N)]
        t[:, g], u[:, g] = grow(rng, parts, lines)
    pos = np.argsort(rng.random((N, 8, 16, 1)), axis=2); th = rng.choice(np.array([0, 1, 7, 100, 253, 254]), (N, 8, 16, 1))
    low = np.floor(rng.random((N, 8, 16, 1)) * (255 - th)).astype(np.int64); step = th + (pos >= VO - 1).astype(np.int64)
    x = low + step * rng.integers(0, 2, (N, 8, 1, V))
    for r in range(N):
        for q in range(8):
            g = int(o[q]); s = np.argsort(u[r, g])[t[(r + 1) % N, g][u[r, g]]]; row, first = orbits(t[r, g][s]); size = np.diff(np.append(first, V))
            i = int(np.argmax(pos[r, g, :, 0] == VO - 1)); a = int(low[r, g, i, 0]); b = int(th[r, g, i, 0])
            if q < 3:
                k = int(np.argmax(size)); n = int(size[k]) // 2; j = n - 1 if q == 1 else int(rng.integers(V // 3, n))
                x[r, g, i] = a; x[r, g, i, int(row[int(first[k]) + j + n * int(rng.integers(0, 2))])] = a + b + (r + q) % 2
            else:
                k = int(np.flatnonzero(size % 2 == 0)[-1]); v = int(row[first[k]]); w = int(row[first[k] + 1])
                x[r, g, :, v] = low[r, g, :, 0]; x[r, g, :, w] = low[r, g, :, 0] + step[r, g, :, 0]; x[r, g, i, w] = a + b
    return pack(t, u, x, th)
def setup_inputs_votes(rng):
    t, u = base(rng); x, th = hang(rng)
    return pack(t, u, x, th)
def check_inputs(d):
    bad = []
    for k, lo, hi in (("t0", 0, V - 1), ("u0", 0, V - 1), ("x", 0, 255), ("th", 0, 255)):
        a = np.asarray(d[k]).astype(np.float64)
        if not (np.min(a) >= lo and np.max(a) <= hi): bad.append("range of " + k)
        elif np.any(a != np.floor(a)): bad.append("whole numbers in " + k)
    if not bad:
        t = np.stack([gentries(a) for a in np.asarray(d["t0"])]).astype(np.int64); u = np.stack([gentries(a) for a in np.asarray(d["u0"])]).astype(np.int64)
        if np.any(np.take_along_axis(t, t, 2) != np.arange(V)): bad.append("t0 holds involutions")
        if np.any(np.sort(u, axis=2) != np.arange(V)): bad.append("u0 holds permutations")
    return bad
def orbits(c):
    c = c.tolist(); seen = bytearray(V); row = []; first = []
    for v in range(V):
        if not seen[v]:
            first.append(len(row))
            while not seen[v]:
                seen[v] = 1; row.append(v); v = c[v]
    return np.array(row), np.array(first)
def reference(t0, u0, x, th):
    t = np.stack([gentries(a) for a in t0]).astype(np.int64); u = np.stack([gentries(a) for a in u0]).astype(np.int64)
    xs = x.astype(np.float32).reshape(N, 8, 16, V); lim = th.astype(np.float32).reshape(N, 8, 16, 1)
    for rnd in range(RO):
        tn = np.empty_like(t); un = np.empty_like(u)
        for r in range(N):
            for g in range(8):
                far = t[(r + 1) % N, g]
                s = np.argsort(u[r, g])[far[u[r, g]]]; c = t[r, g][s]
                row, first = orbits(c); size = np.diff(np.append(first, V))
                start = np.repeat(first, size); o = np.repeat(size, size)
                half = row[start + (np.arange(V) - start + o // 2) % o]
                gap = np.abs(xs[r, g][:, row] - xs[r, g][:, half])
                top = np.maximum.reduceat(gap, first, axis=1)
                votes = np.add.reduce((top <= lim[r, g]).astype(np.int64), axis=0)
                turn = np.repeat((size % 2 == 1) | (votes >= VO), size)
                k = np.empty(V, np.int64); k[row] = np.where(turn, half, row)
                h = u[r, g][k]
                tn[r, g] = np.argsort(h)[far[h]]; un[(r + 1) % N, (g + GS) % 8] = h
        t, u = tn, un
    return {"yt": np.stack([gtable(a) for a in t]).astype(np.float32), "yu": np.stack([gtable(a) for a in u]).astype(np.float32)}

@@ -1,0 +1,510 @@
+from concourse.bass import DstId, RemoteDMATransfer
+from concourse.mybir import dt, AluOpType as OP, AxisListType, ActivationFunctionType as AF
+
+V = 1536
+W = V // 16
+NCH = 3
+CH = V // NCH
+CW = CH // 16
+GCONV = 320
+VSH = 288
+NSTEP = 11
+BIG = 4096.0
+M1 = 1.5 * 2.0 ** 23
+
+
+def _f(n):
+    return ("sbuf", [128, n], "float32")
+
+
+def _b(n):
+    return ("sbuf", [128, n], "bfloat16")
+
+
+def _u(n):
+    return ("sbuf", [128, n], "uint16")
+
+
+def _i(n):
+    return ("sbuf", [128, n], "int32")
+
+
+SCRATCH = {
+    "X0": _f(V), "X1": _f(V), "Y": _f(V), "Al": _f(V), "Be": _f(V), "Tt": _f(V), "Iw": _f(V), "Ic": _f(V),
+    "Xb": _b(V), "Xb0": _b(V), "Ub": _b(V), "R": _b(V), "Gl": _b(V), "Gs": _b(V), "Z": _b(V), "Gh": _b(V),
+    "Ga": _b(V), "Gb": _b(V), "xin": _b(V), "xlo": _b(768), "df": _b(768), "ad": _b(768), "Mx": _b(784),
+    "D": ("sbuf", [128, 8, 16, 16], "bfloat16"),
+    "ti": _i(W), "ui": _i(W), "thi": _i(4), "thf": _f(4), "thb": _f(4),
+    "tl0": _u(W), "tl1": _u(W), "ul0": _u(W), "ul1": _u(W), "fl0": _u(W), "fl1": _u(W), "hs": _u(W),
+    "hf": _f(W), "yl": _f(W), "tW0": _f(W), "tW1": _f(W), "tW2": _f(W),
+    "Lc": _u(W), "Ls": _u(W), "Ll": _u(W), "Lp": _u(W), "Lq": _u(W), "Le": _u(W), "Lf": _u(W), "Lo": _u(W),
+    "sW": _f(W), "uW": _f(W), "nW": _f(W), "eW": _f(W), "w1": _f(W), "w2": _f(W), "w3": _f(W), "w4": _f(W),
+    "w5": _f(W), "w6": _f(W), "w7": _f(W), "w8": _f(W), "w9": _f(W), "vW": _f(W),
+    "pi": _i(16), "pm": _i(16), "col": _f(16), "yb": _f(16), "ia": _f(8), "ib": _f(256), "A1": _f(8), "A2": _f(8),
+    "B1": _f(256), "B2": _f(256),
+    "cb": _b(1408), "cf": _f(512), "v2": _f(128), "rst": _f(128),
+    "D0": _f(128), "oi": _i(128), "pr": _i(128), "wv": _f(128), "E": _f(128), "Sc": _f(128), "rD": _f(128),
+    "dm": _f(128), "oo": _f(128), "ne": _f(128), "R0": _f(128), "Rc": _f(128), "dA": _f(128), "dB": _f(128),
+    "dC": _f(128), "d2": _f(128), "m1": _f(128), "Y1": _f(128), "Q1": _f(128), "Q2": _f(128), "Q3": _f(128),
+    "Q4": _f(128), "Q5": _f(128), "hi": _f(128), "e1": _f(128), "e2": _f(128), "nU": _f(128),
+}
+for _k in range(8):
+    SCRATCH["p%d" % _k] = ("psum", [128, 512], "float32")
+
+SEMAPHORES = ["sv", "ss", "sg", "sp", "ldt", "ldu", "ldx", "ldh", "st0", "st1", "sent", "aT0", "aT1", "aH0", "aH1"]
+
+WC, WS, WB, WU, WA, WH, FB, IB, SD0, SD3, ST = 0, 160, 320, 480, 640, 800, 960, 1088, 1216, 1232, 1248
+IF, IS, ON, TR, SK = 0, 128, 224, 320, 416
+
+
+def relay_of(T, topo, core):
+    n = len(T.cores)
+    need = []
+    for r, c in enumerate(T.cores):
+        if c in topo.cores_of(core):
+            need += [d for d in (T.cores[(r - 1) % n], T.cores[(r + 1) % n]) if not topo.may_write(c, d)]
+    ok = [c for c in topo.cores_of(core) if c not in T.cores and all(topo.may_write(c, d) for d in need)]
+    return ok[0] if need else None
+
+
+def emask(topo, src, dst, far):
+    n = len(topo.engines(src, dst)) if far is None else len(topo.engines(far[0], far[1]))
+    n = min(n, 8)
+    return sum(1 << e for e in topo.engines(src, dst)[:n]), n
+
+
+def relay_program(g, core, T, topo):
+    n = len(T.cores)
+    jobs = []
+    for name, buf, step in (("aT0", "fl0", -1), ("aH0", "ul1", 1), ("aT1", "fl1", -1), ("aH1", "yl", 1)):
+        for r, c in enumerate(T.cores):
+            d = T.cores[(r + step) % n]
+            if c in topo.cores_of(core) and not topo.may_write(c, d):
+                jobs.append((name, buf, c, d))
+    total = 0
+    for name, buf, c, d in jobs:
+        g.wait_ge(T.sem[name], emask(topo, c, core, None)[1])
+        m, k = emask(topo, core, d, None)
+        rid, pid = topo.addr(d, core)
+        g.remote_dma(T[buf][:], T[buf][:], T.sem[name], T.sem.sent, pid, rid, m)
+        total += k
+    g.wait_ge(T.sem.sent, total)
+
+
+def rank_program(g, core, T, topo):
+    rank = T.rank_of(core)
+    if rank is None:
+        if any(c in T.cores for c in topo.cores_of(core)) and relay_of(T, topo, core) == core:
+            relay_program(g, core, T, topo)
+        return
+    n = len(T.cores)
+    Q = {"v": g.vector, "s": g.scalar, "g": g, "p": g.tensor, "y": g.sync}
+    SEM = {"v": "sv", "s": "ss", "g": "sg", "p": "sp"}
+    cnt = {}
+    clock = {q: {} for q in Q}
+    tokclock = {}
+    writer = {}
+    readers = {}
+
+    def need(q, tok):
+        s, c = tok
+        if clock[q].get(s, 0) >= c:
+            return
+        Q[q].wait_ge(T.sem[s], c)
+        for k, x in tokclock[tok].items():
+            if clock[q].get(k, 0) < x:
+                clock[q][k] = x
+
+    def mark(tok, q, rd, wr):
+        ck = dict(clock[q]) if q else {}
+        ck[tok[0]] = tok[1]
+        tokclock[tok] = ck
+        for k in rd:
+            readers.setdefault(k, []).append(tok)
+        for k in wr:
+            writer[k] = tok
+            readers[k] = []
+
+    def deps(q, rd, wr):
+        own = SEM.get(q)
+        ts = []
+        for k in rd:
+            if k in writer:
+                ts.append(writer[k])
+            if k[0] == "#":
+                ts += [t for t in readers.get(k, []) if t[0] != own]
+        for k in wr:
+            if k in writer and not (q == "p" and writer[k][0] == own):
+                ts.append(writer[k])
+            ts += [t for t in readers.get(k, []) if not (q == "p" and t[0] == own)]
+        best = {}
+        for s, c in ts:
+            best[s] = max(best.get(s, 0), c)
+        for s, c in sorted(best.items(), key=lambda z: z[0] == own):
+            need(q, (s, c))
+
+    def op(q, fn, rd, wr):
+        deps(q, rd, wr)
+        r = fn()
+        s = SEM[q]
+        for x in (r if isinstance(r, list) else [r]):
+            x.then_inc(T.sem[s], 1)
+            cnt[s] = cnt.get(s, 0) + 1
+        mark((s, cnt[s]), q, rd, wr)
+
+    def dma(q, out, in_, sem, rd, wr, **kw):
+        deps(q, rd, wr)
+        Q[q].dma_start(out, in_, **kw).then_inc(T.sem[sem], 16)
+        cnt[sem] = 16
+        mark((sem, 16), q, rd, wr)
+
+    def send(src, skey, buf, sem, step):
+        d = T.cores[(rank + step) % n]
+        if not topo.may_write(core, d):
+            d = relay_of(T, topo, core)
+        deps("g", [skey], [])
+        m, k = emask(topo, core, d, None)
+        rid, pid = topo.addr(d, core)
+        g.remote_dma(T[buf][:], src, T.sem[sem], T.sem.sent, pid, rid, m)
+        cnt["sent"] = cnt.get("sent", 0) + k
+
+    for sem, buf, step in (("aT0", "fl0", 1), ("aT1", "fl1", 1), ("aH0", "ul1", -1), ("aH1", "yl", -1)):
+        c = T.cores[(rank + step) % n]
+        if not topo.may_write(c, core):
+            c = relay_of(T, topo, c)
+        k = emask(topo, c, core, None)[1]
+        cnt[sem] = k
+        mark((sem, k), None, [], [buf])
+
+    vec, act, pe = g.vector, g.scalar, g.tensor
+
+    def ts(out, in0, s1, s2, o0, o1, rd, wr):
+        if o1 is None:
+            op("v", lambda: vec.tensor_scalar(out, in0, s1, None, o0), rd, wr)
+        else:
+            op("v", lambda: vec.tensor_scalar(out, in0, s1, s2, o0, o1), rd, wr)
+
+    def tt(out, a, b, o, rd, wr):
+        op("v", lambda: vec.tensor_tensor(out, a, b, o), rd, wr)
+
+    def cp(out, a, rd, wr):
+        op("v", lambda: vec.tensor_copy(out, a), rd, wr)
+
+    def sa(out, a, func, rd, wr, bias=0.0, scale=1.0):
+        op("s", lambda: act.activation(out, a, func, bias=bias, scale=scale), rd, wr)
+
+    def ck(name, a=0, b=V):
+        return ["%s:%d" % (name, j) for j in range(a // 32, (b + 31) // 32)]
+
+    def gather2(out, win, wcols, lst, split, a=0, b=V):
+        m = a + split
+        wk = ck(win, 0, wcols)
+        cp(T[out][:, a:m], T[win][:, 0:wcols].indirect(T[lst][:, a // 16:m // 16]), wk + [lst], ck(out, a, m))
+        sa(T[out][:, m:b], T[win][:, 0:wcols].indirect(T[lst][:, m // 16:b // 16]), AF.Identity, wk + [lst], ck(out, m, b))
+
+    def wrap(bank, c0, base, src, a, b, step, off, rd):
+        nn = (b - a) // step
+        mul = step // 16
+        op("p", lambda: [pe.matmul(T[bank][:, c0:c0 + nn], T.cb[:, base + 16 - i:base + 144 - i],
+                                   T[src][:, a + mul * i + off:b:step], i == 0, i == 15) for i in range(16)],
+           rd + ["cb%d" % base], ["#" + bank])
+
+    def turn(bank, c0, ncol, sel, skey, src, rd, m0=0, m1=W):
+        op("p", lambda: [pe.matmul(T[bank][m0:m1, c0 + i:c0 + 16 * ncol:16], T[src][:, 16 * m0 + i:16 * m1:16], sel, True, True)
+                         for i in range(16)], rd + [skey], ["#" + bank])
+
+    def flip(bank, c0, srcs, extra=None):
+        calls = [(T[s][0:W, :], T.cf[0:W, idc:idc + W]) for s, idc in srcs]
+        rd = [s for s, idc in srcs] + ["cfI", "cfS"]
+        if extra:
+            calls = [(T.cf[:, IF:IF + 128], T[extra][:, :])] + calls
+            rd.append(extra)
+        op("p", lambda: [pe.matmul(T[bank][:, c0:c0 + W], a, b, j == 0, j == len(calls) - 1) for j, (a, b) in enumerate(calls)],
+           rd, ["#" + bank])
+
+    dma("y", T.ti[:], T.t0[:], "ldt", [], ["ti"])
+    dma("s", T.ui[:], T.u0[:], "ldu", [], ["ui"])
+    dma("y", T.xin[:], T.x[:], "ldx", [], ck("xin"))
+
+    def iota(out, pat, base, cm, wr, flt=True):
+        if flt:
+            op("g", lambda: g.iota(out, pat, base, cm, allow_small_or_imprecise_dtypes=True), [], wr)
+        else:
+            op("g", lambda: g.iota(out, pat, base, cm), [], wr)
+
+    def put(ap, pat, base, val, key, cm=1):
+        op("g", lambda: g.affine_select(ap, ap, pat, OP.not_equal, val, base, cm), [key], [key])
+
+    iota(T.pi[:, 0:1], [[0, 1]], 0, 1, ["pi"], False)
+    iota(T.ia[:, 0:6], [[256, 6]], 0, 0, ["ia"])
+    iota(T.ib[:, :], [[1, 256]], 0, 0, ["ib"])
+    cbkeys = ["cb%d" % b for b in (WC, WS, WB, WU, WA, WH, FB, IB, SD0, SD3)] + ["st%d" % j for j in range(8)]
+    ts(T.pm[:, 0:1], T.pi[:, 0:1], 15, None, OP.bitwise_and, None, ["pi"], ["pm"])
+    op("v", lambda: vec.memset(T.cb[:], 0.0), [], cbkeys)
+    col = lambda j: T.col[:, j:j + 1]
+    ts(col(0), T.pm[:, 0:1], 2, 2048.0, OP.is_equal, OP.mult, ["pm"], ["c0"])
+    ts(col(1), T.pm[:, 0:1], 2, 768.0, OP.is_equal, OP.mult, ["pm"], ["c1"])
+    ts(col(2), T.pm[:, 0:1], 3, None, OP.is_equal, None, ["pm"], ["c2"])
+    ts(col(3), T.pm[:, 0:1], 4, None, OP.is_equal, None, ["pm"], ["c3"])
+    ts(col(5), T.pm[:, 0:1], 0, col(0), OP.is_equal, OP.add, ["pm", "c0"], ["c5"])
+    ts(col(6), T.pm[:, 0:1], 1, col(0), OP.is_equal, OP.add, ["pm", "c0"], ["c6"])
+    ts(col(4), T.pm[:, 0:1], 2, None, OP.is_equal, None, ["pm"], ["c4"])
+    ts(T.A1[:, 0:6], T.ia[:, 0:6], col(5), col(1), OP.mult, OP.add, ["ia", "c5", "c1"], ["A1"])
+    ts(T.B1[:, :], T.ib[:, :], col(6), None, OP.mult, None, ["ib", "c6"], ["B1"])
+    sa(T.A2[:, 0:6], T.ia[:, 0:6], AF.Identity, ["ia", "c2"], ["A2"], scale=col(2))
+    sa(T.B2[:, :], T.ib[:, :], AF.Identity, ["ib", "c3"], ["B2"], scale=col(3))
+    for a in range(6):
+        k = (256 * a, 256 * a + 256)
+        sa(T.Ic[:, k[0]:k[1]], T.B2[:, :], AF.Identity, ["A2", "B2"], ck("Ic", *k), bias=T.A2[:, a:a + 1])
+        if a == 3:
+            cp(T.tl0[:], T.ti[:], ["ti"], ["tl0"])
+        ts(T.Iw[:, k[0]:k[1]], T.B1[:, :], T.A1[:, a:a + 1], None, OP.add, None, ["A1", "B1"], ck("Iw", *k))
+    cp(T.ul0[:], T.ui[:], ["ui"], ["ul0"])
+    g8 = [[-16, 8]]
+    wv = lambda b: T.cb[:, b + 16:b + 144:16]
+    put(wv(WC), g8, 0, 1.0, "cb%d" % WC)
+    put(T.cb[:, SD0:SD0 + 8], g8, 0, 1.0, "cb%d" % SD0)
+    put(wv(WC), g8, -1, 1.0, "cb%d" % WC)
+    put(T.cb[:, SD0 + 8:SD0 + 16], g8, -1, 1.0, "cb%d" % SD0)
+    send(T.tl0[:], "tl0", "fl0", "aT0", -1)
+    dma("g", T.thi[:, 0:1], T.th[:], "ldh", [], ["thi"], allow_slow_non_contiguous=True)
+
+    def consts_v():
+        op("v", lambda: vec.memset(T.cf[:], 0.0), [], ["cfI", "cfS", "cfO", "cfT", "cfK"])
+        op("v", lambda: vec.memset(T.cf[:, ON:ON + W], 1.0), [], ["cfO"])
+        op("v", lambda: vec.memset(T.cf[:, TR:TR + W], -1.0), [], ["cfT"])
+        op("v", lambda: vec.memset(wv(WA), 1.0), [], ["cb%d" % WA])
+        op("v", lambda: vec.memset(T.rst[:], 1.0), [], ["rst"])
+        op("v", lambda: vec.memset(T.rst[:, 0:128:16], 0.0), [], ["rst"])
+        op("v", lambda: vec.memset(T.Mx[:, 768:784], 0.0), [], ["Mx:24"])
+
+    def consts_g():
+        tabs = [[(8, -1.0), (9, -1.0)],
+                [(10, 4096.0), (11, 4096.0), (12, 1.0), (13, 1.0), (2, 1.0), (8, 1.0), (9, 1.0)],
+                [(2, 1.0), (12, 1.0), (13, 1.0)], [(2, 1.0)],
+                [(12, -1.0), (13, -1.0), (14, 1.0), (15, 1.0)], [(14, 0.5), (15, 0.5), (2, 0.5)],
+                [(14, -1.0), (15, -1.0), (2, -2.0)], [(10, 2048.0), (11, 2048.0)]]
+        jobs = [[(T.cb[:, ST + 8 * j:ST + 8 * j + 8], g8, -t, w, "st%d" % j) for t, w in tab] for j, tab in enumerate(tabs)]
+        jobs.append([(wv(WS), g8, -t, 1.0, "cb%d" % WS) for t in (3, 4)])
+        jobs.append([(T.cb[:, SD3 + 8 * (t - 3):SD3 + 8 * (t - 2)], g8, -t, 1.0, "cb%d" % SD3) for t in (3, 4)])
+        jobs.append([(wv(WB), g8, -t, 2048.0, "cb%d" % WB) for t in (10, 11)])
+        jobs.append([(T.cb[:, WU + 32:WU + 144:16], [[-16, 7]], -t, 1.0, "cb%d" % WU) for t in (5, 6)]
+                    + [(T.cb[:, WU + 16:WU + 17], [[0, 1]], -112 - t, 1.0, "cb%d" % WU) for t in (5, 6)])
+        jobs.append([(T.cb[:, FB:FB + 128], [[-16, 8], [0, 16]], -7, 1.0, "cb%d" % FB)])
+        jobs.append([(T.cb[:, IB:IB + 128], [[-1, 128]], 0, 1.0, "cb%d" % IB)])
+        jobs.append([(T.cf[:, IF:IF + 128], [[-1, 128]], 0, 1.0, "cfI")])
+        jobs.append([(T.cf[:, IS:IS + W], [[-1, W]], 0, 1.0 / 2048, "cfS")])
+        jobs.append([(T.cf[:, SK:SK + 8], g8, -2, 1.0, "cfK")])
+        jobs = jobs[9:10] + jobs[8:9] + jobs[10:] + jobs[:8]
+        while any(jobs):
+            for j in jobs:
+                if j:
+                    put(*j.pop(0))
+        k = "cb%d" % WA
+        op("g", lambda: g.affine_select(wv(WA), wv(WA), g8, OP.is_ge, 0.0, 0, 1), [k], [k])
+        op("g", lambda: g.affine_select(T.cf[:, TR:TR + W], T.cf[:, TR:TR + W], [[-1, W]], OP.is_gt, 0.0, 0, 1), ["cfT"], ["cfT"])
+        op("g", lambda: g.affine_select(wv(WA), wv(WA), [[16, 8]], OP.is_ge, 0.0, 15, -1), [k], [k])
+        iota(T.v2[:, :], [[0, 8], [2048, 16]], 0, 32768, ["v2"])
+        iota(T.vW[:, :], [[16, W]], 0, 0, ["vW"])
+        iota(T.Q1[:, :], [[0, 8], [1, 16]], 0, 16, ["Q1"])
+
+    def consts_s():
+        sa(T.cb[:, WH + 32:WH + 144:16], T.cb[:, WA + 16:WA + 128:16], AF.Identity, ["cb%d" % WA], ["cb%d" % WH])
+        sa(T.cb[:, WH + 16:WH + 17], T.cb[:, WA + 128:WA + 129], AF.Identity, ["cb%d" % WA], ["cb%d" % WH])
+        sa(T.D[0:W, :, 0, :], T.Q1[0:W, :], AF.Identity, ["Q1"], ["D0_"])
+
+    def consts_late():
+        tt(T.D[0:W, :, 1, :], T.Q1[0:W, :], T.D[0:W, :, 0, :], OP.subtract, ["Q1", "D0_"], ["D1_"])
+        cp(col(7), T.pm[:, 0:1], ["pm"], ["c7"])
+        ts(T.vW[:, :], T.vW[:, :], col(7), None, OP.add, None, ["vW", "c7"], ["vW"])
+        cp(T.thf[:, 0:1], T.thi[:, 0:1], ["thi"], ["thf"])
+        cp(T.tW0[:], T.ti[:], ["ti"], ["tW0"])
+        sa(T.thb[:, 0:1], T.thf[:, 0:1], AF.Identity, ["thf"], ["thb"], bias=0.5)
+
+    Dk = lambda *t: ["D%d_" % j for j in t]
+    U = lambda name: T[name][0:W, :]
+    P = lambda b, j: T[b][0:W, 128 * j:128 * j + 128]
+
+    def after(k, X, j, rnd):
+        a, b = CH * j, CH * j + CH
+        if k <= 9:
+            xb = "Xb0" if k == 0 else "Xb"
+            m = a + GCONV
+            sa(T[xb][:, m:b], T[X][:, m:b], AF.Identity, ck(X, m, b), ck(xb, m, b))
+            if GCONV:
+                op("g", lambda: g.affine_select(T[xb][:, a:m], T[X][:, a:m], [[0, GCONV]], OP.is_ge, 0.0, 0, 0), ck(X, a, m), ck(xb, a, m))
+            wrap("p%d" % j, 0, WC, xb, a, b, 16, 0, ck(xb, a, b))
+        if k < NSTEP:
+            sa(T.Y[:, a:b], T[X][:, a:b], AF.Identity, ck(X, a, b) + ["c4", "yb"], ck("Y", a, b), bias=T.yb[:, min(k, 9):min(k, 9) + 1], scale=col(4))
+
+    for rnd in range(2):
+        tl, ul, fl, tW, tN = "tl%d" % rnd, "ul%d" % rnd, "fl%d" % rnd, "tW%d" % rnd, "tW%d" % (rnd + 1)
+        gather2("Tt", "Iw", V, tl, 768)
+        tt(T.Al[:, :].indirect(T[ul][:, :]), T.Tt[:, :], T.Ic[:, :], OP.add, ck("Tt") + ck("Ic") + [ul], ck("Al"))
+        if rnd == 0:
+            consts_v()
+            consts_g()
+            for k in range(10):
+                sa(T.yb[:, k:k + 1], col(4), AF.Identity, ["c4"], ["yb"], bias=BIG, scale=-BIG - 2.0 ** k)
+        sa(T.Ub[:, :], T.Iw[:, :].indirect(T[ul][:, :]), AF.Identity, ck("Iw") + [ul], ck("Ub"))
+        turn("p6", 0, 16, T.cb[:, SD0:SD0 + 16], "cb%d" % SD0, "Ub", ck("Ub"))
+        sa(T.D[0:W, :, 5, :], P("p6", 0), AF.Identity, ["#p6"], Dk(5))
+        sa(T.D[0:W, :, 6, :], P("p6", 1), AF.Identity, ["#p6"], Dk(6))
+        gather2("Be", "Al", V, fl, 768)
+        for j in range(NCH):
+            gather2("X0", "Be", V, ul, VSH, CH * j, CH * j + CH)
+        for j in range(NCH):
+            after(0, "X0", j, rnd)
+        for k in range(NSTEP):
+            X, Xn = ("X0", "X1") if k % 2 == 0 else ("X1", "X0")
+            for j in range(NCH):
+                a, b = CH * j, CH * j + CH
+                lk = "Lc%d" % j
+                if k <= 9:
+                    cp(T.Lc[:, CW * j:CW * j + CW], T["p%d" % j][:, 0:CW], ["#p%d" % j], [lk])
+                tt(T[Xn][:, a:b], T[X][:, :].indirect(T.Lc[:, CW * j:CW * j + CW]), T.Y[:, a:b], OP.min,
+                   ck(X) + [lk] + ck("Y", a, b), ck(Xn, a, b))
+                after(k + 1, Xn, j, rnd)
+                if k == NSTEP - 1:
+                    turn("p3", 0, 8, T.cf[:, SK:SK + 8], "cfK", Xn, ck(Xn, a, b), CW * j, CW * j + CW)
+            if k == 8 and rnd == 0:
+                consts_s()
+            if k == 9:
+                wrap("p6", 0, WS, "Xb0", 0, V, 16, 0, ck("Xb0"))
+                turn("p7", 0, 16, T.cb[:, SD3:SD3 + 16], "cb%d" % SD3, "Xb0", ck("Xb0"))
+                sa(T.sW[:, :], T.p6[:, 0:W], AF.Identity, ["#p6"], ["sW"])
+                sa(T.D[0:W, :, 3, :], P("p7", 0), AF.Identity, ["#p7"], Dk(3))
+                sa(T.D[0:W, :, 4, :], P("p7", 1), AF.Identity, ["#p7"], Dk(4))
+                if rnd == 0:
+                    consts_late()
+        M2 = M1 * 2048
+        tt(U("D0"), P("p3", 0), U("v2"), OP.subtract, ["#p3", "v2"], ["D0"])
+        ts(U("oi"), U("D0"), 768.0, 0.0, OP.add, OP.max, ["D0"], ["oi"])
+        ts(U("rD"), U("D0"), M2, -M2, OP.add, OP.add, ["D0"], ["rD"])
+        ts(U("pr"), U("oi"), 1, None, OP.bitwise_and, None, ["oi"], ["pr"])
+        flip("p5", 0, [("rD", IS)], "vW")
+        ts(U("wv"), U("pr"), 1.0 - 2.0 ** -12, 2.0 ** -12, OP.mult, OP.add, ["pr"], ["wv"])
+        tt(U("oo"), U("oi"), U("pr"), OP.mult, ["oi", "pr"], ["oo"])
+        tt(U("E"), U("oi"), U("wv"), OP.mult, ["oi", "wv"], ["E"])
+        sa(T.D[0:W, :, 2, :], U("wv"), AF.Sign, ["wv"], Dk(2), bias=1.0, scale=-1.0)
+        sa(T.D[0:W, :, 14, :], U("oo"), AF.Identity, ["oo"], Dk(14))
+        tt(U("ne"), U("oo"), U("oi"), OP.subtract, ["oi", "oo"], ["ne"])
+        op("v", lambda: vec.tensor_tensor_scan(U("Sc"), U("rst"), U("E"), 0.0, OP.mult, OP.add), ["rst", "E"], ["Sc"])
+        op("p", lambda: [pe.matmul(P("p4", 0), T.cf[0:W, TR:TR + W], U("E"), True, False)], ["cfT", "E"], ["#p4"])
+        op("p", lambda: [pe.matmul(P("p4", 0), T.cf[0:W, ON:ON + W], U("Sc"), False, True)], ["cfO", "Sc"], ["#p4"])
+        sa(T.D[0:W, :, 12, :], U("ne"), AF.Identity, ["ne"], Dk(12))
+        tt(U("dm"), U("D0"), U("rD"), OP.subtract, ["D0", "rD"], ["dm"])
+        tt(T.D[0:W, :, 15, :], U("oo"), T.D[0:W, :, 14, :], OP.subtract, ["oo"] + Dk(14), Dk(15))
+        tt(T.D[0:W, :, 13, :], U("ne"), T.D[0:W, :, 12, :], OP.subtract, ["ne"] + Dk(12), Dk(13))
+        sa(T.D[0:W, :, 7, :], U("dm"), AF.Sign, ["dm"], Dk(7), bias=767.0)
+        ts(T.D[0:W, :, 8, :], P("p4", 0), M1 * 64, -M1 * 64, OP.add, OP.add, ["#p4"], Dk(8))
+        ts(U("R0"), P("p4", 0), M1, -M1, OP.add, OP.add, ["#p4"], ["R0"])
+        ts(U("Rc"), P("p4", 0), M1 / 32, -M1 / 32, OP.add, OP.add, ["#p4"], ["Rc"])
+        tt(T.D[0:W, :, 9, :], U("R0"), T.D[0:W, :, 8, :], OP.subtract, ["R0"] + Dk(8), Dk(9))
+        tt(T.D[0:W, :, 10, :], U("Rc"), U("R0"), OP.subtract, ["R0", "Rc"], Dk(10))
+        tt(T.D[0:W, :, 11, :], P("p4", 0), U("Rc"), OP.subtract, ["#p4", "Rc"], Dk(11))
+        cp(T.Ll[:, :], T.p5[:, 0:W], ["#p5"], ["Ll"])
+        cp(T.Ls[:, :], T.sW[:, :], ["sW"], ["Ls"])
+        sa(U("dA"), U("dm"), AF.Identity, ["dm"], ["dA"], bias=768.0 + 1535.0)
+        sa(U("dB"), U("dm"), AF.Identity, ["dm"], ["dB"], bias=768.0 - 1538.0)
+        sa(U("dC"), U("dm"), AF.Identity, ["dm"], ["dC"], bias=1.0 - 1536.0, scale=-2.0)
+        sa(U("d2"), U("dm"), AF.Identity, ["dm"], ["d2"], bias=1536.0, scale=2.0)
+        for b in range(3):
+            op("p", lambda: [pe.matmul(T["p%d" % b][:, i:512:16], T.D[0:W, :, :, i], T.cb[0:W, IB + 32 * b:IB + 32 * b + 32], True, True)
+                             for i in range(16)], Dk(*range(16)) + ["cb%d" % IB], ["#p%d" % b])
+        sa(T.R[:, 0:512], T.p0[:, :], AF.Identity, ["#p0"], ck("R", 0, 512))
+        cp(T.R[:, 512:1024], T.p1[:, :], ["#p1"], ck("R", 512, 1024))
+        sa(T.R[:, 1024:1536], T.p2[:, :], AF.Identity, ["#p2"], ck("R", 1024, 1536))
+        gather2("Gl", "R", V, "Ll", 768)
+        turn("p3", 0, 32, T.cb[:, ST:ST + 32], "st0", "Gl", ck("Gl") + ["st1", "st2", "st3"])
+        turn("p4", 0, 32, T.cb[:, ST + 32:ST + 64], "st4", "Gl", ck("Gl") + ["st5", "st6", "st7"])
+        tt(U("m1"), P("p3", 2), U("dC"), OP.is_gt, ["#p3", "dC"], ["m1"])
+        tt(U("Y1"), P("p3", 1), U("dB"), OP.add, ["#p3", "dB"], ["Y1"])
+        tt(U("Q1"), P("p3", 0), U("dA"), OP.add, ["#p3", "dA"], ["Q1"])
+        tt(U("Q2"), P("p3", 2), U("m1"), OP.mult, ["#p3", "m1"], ["Q2"])
+        tt(U("Q3"), P("p3", 3), U("Y1"), OP.mult, ["#p3", "Y1"], ["Q3"])
+        flip("p5", 0, [("Q1", IF), ("Q2", IF), ("Q3", IF)])
+        tt(U("hi"), P("p4", 0), U("d2"), OP.is_lt, ["#p4", "d2"], ["hi"])
+        tt(U("Q4"), P("p4", 2), U("hi"), OP.mult, ["#p4", "hi"], ["Q4"])
+        cp(T.Lp[:, :], T.p5[:, 0:W], ["#p5"], ["Lp"])
+        cp(T.Z[:, :].indirect(T.Lp[:, :]), T.R[:, :], ck("R") + ["Lp"], ck("Z"))
+        sa(U("Q5"), P("p4", 1), AF.Identity, ["#p4"], ["Q5"])
+        sa(U("e1"), P("p4", 3), AF.Identity, ["#p4"], ["e1"])
+        sa(U("nU"), P("p3", 3), AF.Identity, ["#p3"], ["nU"])
+        flip("p0", 0, [("Q1", IF), ("Q2", IF), ("Q3", IF), ("Q4", IF), ("Q5", IF)])
+        flip("p3", 0, [("e1", IF)])
+        flip("p3", W, [("nU", IF)])
+        wrap("p6", 0, WU, "R", 0, V, 16, 0, ck("R"))
+        sa(T.Gs[:, :], T.Gl[:, :].indirect(T.Ls[:, :]), AF.Identity, ck("Gl") + ["Ls"], ck("Gs"))
+        wrap("p7", 0, WB, "Gs", 0, V, 16, 0, ck("Gs"))
+        sa(T.w1[:, :], T.p3[:, 0:W], AF.Identity, ["#p3"], ["w1"], bias=-769.0)
+        sa(T.nW[:, :], T.p3[:, W:2 * W], AF.Identity, ["#p3"], ["nW"])
+        sa(T.uW[:, :], T.p6[:, 0:W], AF.Identity, ["#p6"], ["uW"])
+        sa(T.eW[:, :], T.p7[:, 0:W], AF.Identity, ["#p7"], ["eW"], bias=-769.0)
+        wrap("p1", 0, WC, "Z", 0, V, 32, 0, ck("Z"))
+        wrap("p2", 0, WC, "Z", 0, V, 32, 1, ck("Z"))
+        for h in range(2):
+            op("p", lambda: [pe.matmul(T["p%d" % (6 + h)][:, 0:384], T.cb[:, FB:FB + 128], T.Z[:, 768 * h:768 * h + 768:2], True, True)],
+               ck("Z") + ["cb%d" % FB], ["#p%d" % (6 + h)])
+        ts(T.Lq[:, :], T.p0[:, 0:W], 0.5, None, OP.add, None, ["#p0"], ["Lq"])
+        gather2("Gh", "Z", V, "Lq", 768)
+        cp(T.Lo[:, 0:48], T.p1[:, 0:48], ["#p1"], ["Lo0"])
+        cp(T.Lo[:, 48:96], T.p2[:, 0:48], ["#p2"], ["Lo1"])
+        wrap("p5", 0, WU, "Gh", 0, V, 16, 0, ck("Gh"))
+        wrap("p3", 0, WS, "Gh", 0, V, 16, 0, ck("Gh"))
+        for h in range(2):
+            a, b = 384 * h, 384 * h + 384
+            sa(T.xlo[:, a:b], T.xin[:, :].indirect(T.Lo[:, 24 * h:24 * h + 24]), AF.Identity, ck("xin") + ["Lo0"], ck("xlo", a, b))
+        tt(T.w2[:, :], T.w1[:, :], T.nW[:, :], OP.mult, ["w1", "nW"], ["w2"])
+        tt(T.w3[:, :], T.eW[:, :], T.nW[:, :], OP.mult, ["eW", "nW"], ["w3"])
+        ts(T.Le[:, :], T.w2[:, :], 768.0, None, OP.add, None, ["w2"], ["Le"])
+        ts(T.Lf[:, :], T.w3[:, :], 768.0, None, OP.add, None, ["w3"], ["Lf"])
+        for h in range(2):
+            a, b = 384 * h, 384 * h + 384
+            tt(T.df[:, a:b], T.xin[:, :].indirect(T.Lo[:, 48 + 24 * h:72 + 24 * h]), T.xlo[:, a:b], OP.subtract,
+               ck("xin") + ["Lo1"] + ck("xlo", a, b), ck("df", a, b))
+            sa(T.ad[:, a:b], T.df[:, a:b], AF.Abs, ck("df", a, b), ck("ad", a, b))
+        for h in range(2):
+            a, b = 384 * h, 384 * h + 384
+            init = 0.0 if h == 0 else T.Mx[:, a - 1:a]
+            op("v", lambda: vec.tensor_tensor_scan(T.Mx[:, a:b], T["p%d" % (6 + h)][:, 0:384], T.ad[:, a:b], init, OP.mult, OP.max),
+               ["#p%d" % (6 + h)] + ck("ad", a, b) + ck("Mx", 0, a), ck("Mx", a, b))
+
+        def agree(out, lst):
+            wk = ck("Mx", 0, 784)
+            ts(T[out][:, 0:768], T.Mx[:, :].indirect(T[lst][:, 0:48]), T.thf[:, 0:1], 0.5, OP.is_le, OP.subtract,
+               wk + [lst, "thf"], ck(out, 0, 768))
+            sa(T[out][:, 768:V], T.Mx[:, :].indirect(T[lst][:, 48:96]), AF.Sign, wk + [lst, "thb"], ck(out, 768, V),
+               bias=T.thb[:, 0:1], scale=-1.0)
+
+        agree("Ga", "Le")
+        wrap("p1", 0, WH, "Ga", 0, V, 16, 0, ck("Ga"))
+        wrap("p2", 0, WA, "Ga", 0, V, 16, 0, ck("Ga"))
+        tt(T.w4[:, :], T.p5[:, 0:W], T.uW[:, :], OP.subtract, ["#p5", "uW"], ["w4"])
+        agree("Gb", "Lf")
+        wrap("p0", 0, WA, "Gb", 0, V, 16, 0, ck("Gb"))
+        ts(T.w5[:, :], T.p1[:, 0:W], 0.0, None, OP.is_ge, None, ["#p1"], ["w5"])
+        tt(T.w2[:, :], T.sW[:, :], T[tW][:, :], OP.subtract, ["sW", tW], ["w2"])
+        tt(T.w6[:, :], T.w5[:, :], T.w4[:, :], OP.mult, ["w5", "w4"], ["w6"])
+        tt(T.w3[:, :], T.w2[:, :], T.nW[:, :], OP.mult, ["w2", "nW"], ["w3"])
+        tt(T.hf[:, :], T.w6[:, :], T.uW[:, :], OP.add, ["w6", "uW"], ["hf"])
+        tt(T.w7[:, :], T.w3[:, :], T[tW][:, :], OP.add, ["w3", tW], ["w7"])
+        if rnd == 0:
+            cp(T.hs[:, :], T.hf[:, :], ["hf"], ["hs"])
+            send(T.hs[:], "hs", "ul1", "aH0", 1)
+        else:
+            send(T.hf[:], "hf", "yl", "aH1", 1)
+        ts(T.w8[:, :], T.p2[:, 0:W], 0.0, None, OP.is_ge, None, ["#p2"], ["w8"])
+        ts(T.w9[:, :], T.p0[:, 0:W], 0.0, None, OP.is_ge, None, ["#p0"], ["w9"])
+        tt(T.w1[:, :], T.p3[:, 0:W], T.w7[:, :], OP.subtract, ["#p3", "w7"], ["w1"])
+        tt(T.w5[:, :], T.w8[:, :], T.w9[:, :], OP.not_equal, ["w8", "w9"], ["w5"])
+        tt(T.w6[:, :], T.w5[:, :], T.w1[:, :], OP.mult, ["w5", "w1"], ["w6"])
+        tt(T[tN][:, :], T.w6[:, :], T.w7[:, :], OP.add, ["w6", "w7"], [tN])
+        if rnd == 0:
+            cp(T.tl1[:, :], T[tN][:, :], [tN], ["tl1"])
+            send(T.tl1[:], "tl1", "fl1", "aT1", -1)
+    dma("y", T.yt[:], T.tW2[:], "st0", ["tW2"], [])
+    dma("s", T.yu[:], T.yl[:], "st1", ["yl"], [])
+    for s, c in cnt.items():
+        if clock["g"].get(s, 0) < c:
+            g.wait_ge(T.sem[s], c)

@@ -6,7 +6,7 @@ W = V // 16
 NCH = 3
 CH = V // NCH
 CW = CH // 16
-GCONV = 320
+GCONV = 288
 VSH = 288
 NSTEP = 11
 BIG = 4096.0
@@ -240,7 +240,8 @@ def rank_program(g, core, T, topo):
     iota(T.ib[:, :], [[1, 256]], 0, 0, ["ib"])
     cbkeys = ["cb%d" % b for b in (WC, WS, WB, WU, WA, WH, FB, IB, SD0, SD3)] + ["st%d" % j for j in range(8)]
     ts(T.pm[:, 0:1], T.pi[:, 0:1], 15, None, OP.bitwise_and, None, ["pi"], ["pm"])
-    op("v", lambda: vec.memset(T.cb[:], 0.0), [], cbkeys)
+    iota(T.cb[:, WC:WC + 160], [[0, 160]], 0, 0, ["cb%d" % WC])
+    iota(T.cb[:, SD0:SD0 + 16], [[0, 16]], 0, 0, ["cb%d" % SD0])
     col = lambda j: T.col[:, j:j + 1]
     ts(col(0), T.pm[:, 0:1], 2, 2048.0, OP.is_equal, OP.mult, ["pm"], ["c0"])
     ts(col(1), T.pm[:, 0:1], 2, 768.0, OP.is_equal, OP.mult, ["pm"], ["c1"])
@@ -267,18 +268,20 @@ def rank_program(g, core, T, topo):
     put(wv(WC), g8, -1, 1.0, "cb%d" % WC)
     put(T.cb[:, SD0 + 8:SD0 + 16], g8, -1, 1.0, "cb%d" % SD0)
     send(T.tl0[:], "tl0", "fl0", "aT0", -1)
-    dma("g", T.thi[:, 0:1], T.th[:], "ldh", [], ["thi"], allow_slow_non_contiguous=True)
 
     def consts_v():
-        op("v", lambda: vec.memset(T.cf[:], 0.0), [], ["cfI", "cfS", "cfO", "cfT", "cfK"])
-        op("v", lambda: vec.memset(T.cf[:, ON:ON + W], 1.0), [], ["cfO"])
-        op("v", lambda: vec.memset(T.cf[:, TR:TR + W], -1.0), [], ["cfT"])
-        op("v", lambda: vec.memset(wv(WA), 1.0), [], ["cb%d" % WA])
-        op("v", lambda: vec.memset(T.rst[:], 1.0), [], ["rst"])
-        op("v", lambda: vec.memset(T.rst[:, 0:128:16], 0.0), [], ["rst"])
-        op("v", lambda: vec.memset(T.Mx[:, 768:784], 0.0), [], ["Mx:24"])
+        iota(T.cb[:, WS:SD0], [[0, SD0 - WS]], 0, 0, cbkeys[1:8])
+        iota(T.cb[:, SD3:ST + 64], [[0, ST + 64 - SD3]], 0, 0, cbkeys[9:])
+        iota(T.cf[:, IF:ON], [[0, ON - IF]], 0, 0, ["cfI", "cfS"])
+        iota(T.cf[:, ON:ON + W], [[0, W]], 1, 0, ["cfO"])
+        iota(T.cf[:, TR:TR + W], [[0, W]], -1, 0, ["cfT"])
+        iota(T.cf[:, SK:SK + 8], [[0, 8]], 0, 0, ["cfK"])
+        iota(wv(WA), [[0, 8]], 1, 0, ["cb%d" % WA])
+        iota(T.rst[:, :], [[0, 128]], 1, 0, ["rst"])
+        iota(T.Mx[:, 768:784], [[0, 16]], 0, 0, ["Mx:24"])
+        iota(T.rst[:, 0:128:16], [[0, 8]], 0, 0, ["rst"])
 
-    def consts_g():
+    def consts_g(late):
         tabs = [[(8, -1.0), (9, -1.0)],
                 [(10, 4096.0), (11, 4096.0), (12, 1.0), (13, 1.0), (2, 1.0), (8, 1.0), (9, 1.0)],
                 [(2, 1.0), (12, 1.0), (13, 1.0)], [(2, 1.0)],
@@ -295,11 +298,14 @@ def rank_program(g, core, T, topo):
         jobs.append([(T.cf[:, IF:IF + 128], [[-1, 128]], 0, 1.0, "cfI")])
         jobs.append([(T.cf[:, IS:IS + W], [[-1, W]], 0, 1.0 / 2048, "cfS")])
         jobs.append([(T.cf[:, SK:SK + 8], g8, -2, 1.0, "cfK")])
-        jobs = jobs[9:10] + jobs[8:9] + jobs[10:] + jobs[:8]
+        jobs = jobs[:8] + jobs[10:12] if late else jobs[8:10] + jobs[12:]
         while any(jobs):
             for j in jobs:
                 if j:
                     put(*j.pop(0))
+        if late:
+            dma("g", T.thi[:, 0:1], T.th[:], "ldh", [], ["thi"], allow_slow_non_contiguous=True)
+            return
         k = "cb%d" % WA
         op("g", lambda: g.affine_select(wv(WA), wv(WA), g8, OP.is_ge, 0.0, 0, 1), [k], [k])
         op("g", lambda: g.affine_select(T.cf[:, TR:TR + W], T.cf[:, TR:TR + W], [[-1, W]], OP.is_gt, 0.0, 0, 1), ["cfT"], ["cfT"])
@@ -313,13 +319,15 @@ def rank_program(g, core, T, topo):
         sa(T.cb[:, WH + 16:WH + 17], T.cb[:, WA + 128:WA + 129], AF.Identity, ["cb%d" % WA], ["cb%d" % WH])
         sa(T.D[0:W, :, 0, :], T.Q1[0:W, :], AF.Identity, ["Q1"], ["D0_"])
 
-    def consts_late():
+    def consts_late(part):
+        if part:
+            cp(T.thf[:, 0:1], T.thi[:, 0:1], ["thi"], ["thf"])
+            cp(T.tW0[:], T.ti[:], ["ti"], ["tW0"])
+            sa(T.thb[:, 0:1], T.thf[:, 0:1], AF.Identity, ["thf"], ["thb"], bias=0.5)
+            return
         tt(T.D[0:W, :, 1, :], T.Q1[0:W, :], T.D[0:W, :, 0, :], OP.subtract, ["Q1", "D0_"], ["D1_"])
         cp(col(7), T.pm[:, 0:1], ["pm"], ["c7"])
         ts(T.vW[:, :], T.vW[:, :], col(7), None, OP.add, None, ["vW", "c7"], ["vW"])
-        cp(T.thf[:, 0:1], T.thi[:, 0:1], ["thi"], ["thf"])
-        cp(T.tW0[:], T.ti[:], ["ti"], ["tW0"])
-        sa(T.thb[:, 0:1], T.thf[:, 0:1], AF.Identity, ["thf"], ["thb"], bias=0.5)
 
     Dk = lambda *t: ["D%d_" % j for j in t]
     U = lambda name: T[name][0:W, :]
@@ -343,7 +351,7 @@ def rank_program(g, core, T, topo):
         tt(T.Al[:, :].indirect(T[ul][:, :]), T.Tt[:, :], T.Ic[:, :], OP.add, ck("Tt") + ck("Ic") + [ul], ck("Al"))
         if rnd == 0:
             consts_v()
-            consts_g()
+            consts_g(False)
             for k in range(10):
                 sa(T.yb[:, k:k + 1], col(4), AF.Identity, ["c4"], ["yb"], bias=BIG, scale=-BIG - 2.0 ** k)
         sa(T.Ub[:, :], T.Iw[:, :].indirect(T[ul][:, :]), AF.Identity, ck("Iw") + [ul], ck("Ub"))
@@ -351,24 +359,29 @@ def rank_program(g, core, T, topo):
         sa(T.D[0:W, :, 5, :], P("p6", 0), AF.Identity, ["#p6"], Dk(5))
         sa(T.D[0:W, :, 6, :], P("p6", 1), AF.Identity, ["#p6"], Dk(6))
         gather2("Be", "Al", V, fl, 768)
-        for j in range(NCH):
-            gather2("X0", "Be", V, ul, VSH, CH * j, CH * j + CH)
-        for j in range(NCH):
+        gather2("X0", "Be", V, ul, CH // 2, 0, CH)
+        after(0, "X0", 0, rnd)
+        for j in range(1, NCH):
+            cp(T.X0[:, CH * j:CH * j + CH], T.Be[:, :].indirect(T[ul][:, CW * j:CW * j + CW]), ck("Be") + [ul], ck("X0", CH * j, CH * j + CH))
             after(0, "X0", j, rnd)
         for k in range(NSTEP):
             X, Xn = ("X0", "X1") if k % 2 == 0 else ("X1", "X0")
             for j in range(NCH):
                 a, b = CH * j, CH * j + CH
                 lk = "Lc%d" % j
-                if k <= 9:
+                if k == 9 or (k < 9 and j == 0):
                     cp(T.Lc[:, CW * j:CW * j + CW], T["p%d" % j][:, 0:CW], ["#p%d" % j], [lk])
-                tt(T[Xn][:, a:b], T[X][:, :].indirect(T.Lc[:, CW * j:CW * j + CW]), T.Y[:, a:b], OP.min,
-                   ck(X) + [lk] + ck("Y", a, b), ck(Xn, a, b))
+                for c, e in ((a, a + GCONV), (a + GCONV, b)) if k <= 8 else ((a, b),):
+                    if c > a and j + 1 < NCH:
+                        cp(T.Lc[:, CW * (j + 1):CW * (j + 2)], T["p%d" % (j + 1)][:, 0:CW], ["#p%d" % (j + 1)], ["Lc%d" % (j + 1)])
+                    tt(T[Xn][:, c:e], T[X][:, :].indirect(T.Lc[:, c // 16:e // 16]), T.Y[:, c:e], OP.min,
+                       ck(X) + [lk] + ck("Y", c, e), ck(Xn, c, e))
                 after(k + 1, Xn, j, rnd)
                 if k == NSTEP - 1:
                     turn("p3", 0, 8, T.cf[:, SK:SK + 8], "cfK", Xn, ck(Xn, a, b), CW * j, CW * j + CW)
             if k == 8 and rnd == 0:
                 consts_s()
+                consts_g(True)
             if k == 9:
                 wrap("p6", 0, WS, "Xb0", 0, V, 16, 0, ck("Xb0"))
                 turn("p7", 0, 16, T.cb[:, SD3:SD3 + 16], "cb%d" % SD3, "Xb0", ck("Xb0"))
@@ -376,7 +389,7 @@ def rank_program(g, core, T, topo):
                 sa(T.D[0:W, :, 3, :], P("p7", 0), AF.Identity, ["#p7"], Dk(3))
                 sa(T.D[0:W, :, 4, :], P("p7", 1), AF.Identity, ["#p7"], Dk(4))
                 if rnd == 0:
-                    consts_late()
+                    consts_late(0)
         M2 = M1 * 2048
         tt(U("D0"), P("p3", 0), U("v2"), OP.subtract, ["#p3", "v2"], ["D0"])
         ts(U("oi"), U("D0"), 768.0, 0.0, OP.add, OP.max, ["D0"], ["oi"])
@@ -405,6 +418,8 @@ def rank_program(g, core, T, topo):
         tt(T.D[0:W, :, 11, :], P("p4", 0), U("Rc"), OP.subtract, ["#p4", "Rc"], Dk(11))
         cp(T.Ll[:, :], T.p5[:, 0:W], ["#p5"], ["Ll"])
         cp(T.Ls[:, :], T.sW[:, :], ["sW"], ["Ls"])
+        if rnd == 0:
+            consts_late(1)
         sa(U("dA"), U("dm"), AF.Identity, ["dm"], ["dA"], bias=768.0 + 1535.0)
         sa(U("dB"), U("dm"), AF.Identity, ["dm"], ["dB"], bias=768.0 - 1538.0)
         sa(U("dC"), U("dm"), AF.Identity, ["dm"], ["dC"], bias=1.0 - 1536.0, scale=-2.0)
@@ -447,18 +462,13 @@ def rank_program(g, core, T, topo):
             op("p", lambda: [pe.matmul(T["p%d" % (6 + h)][:, 0:384], T.cb[:, FB:FB + 128], T.Z[:, 768 * h:768 * h + 768:2], True, True)],
                ck("Z") + ["cb%d" % FB], ["#p%d" % (6 + h)])
         ts(T.Lq[:, :], T.p0[:, 0:W], 0.5, None, OP.add, None, ["#p0"], ["Lq"])
-        gather2("Gh", "Z", V, "Lq", 768)
+        gather2("Gh", "Z", V, "Lq", 416, 0, 832)
         cp(T.Lo[:, 0:48], T.p1[:, 0:48], ["#p1"], ["Lo0"])
         cp(T.Lo[:, 48:96], T.p2[:, 0:48], ["#p2"], ["Lo1"])
-        wrap("p5", 0, WU, "Gh", 0, V, 16, 0, ck("Gh"))
-        wrap("p3", 0, WS, "Gh", 0, V, 16, 0, ck("Gh"))
+        cp(T.Gh[:, 832:1184], T.Z[:, :].indirect(T.Lq[:, 52:74]), ck("Z") + ["Lq"], ck("Gh", 832, 1184))
         for h in range(2):
             a, b = 384 * h, 384 * h + 384
             sa(T.xlo[:, a:b], T.xin[:, :].indirect(T.Lo[:, 24 * h:24 * h + 24]), AF.Identity, ck("xin") + ["Lo0"], ck("xlo", a, b))
-        tt(T.w2[:, :], T.w1[:, :], T.nW[:, :], OP.mult, ["w1", "nW"], ["w2"])
-        tt(T.w3[:, :], T.eW[:, :], T.nW[:, :], OP.mult, ["eW", "nW"], ["w3"])
-        ts(T.Le[:, :], T.w2[:, :], 768.0, None, OP.add, None, ["w2"], ["Le"])
-        ts(T.Lf[:, :], T.w3[:, :], 768.0, None, OP.add, None, ["w3"], ["Lf"])
         for h in range(2):
             a, b = 384 * h, 384 * h + 384
             tt(T.df[:, a:b], T.xin[:, :].indirect(T.Lo[:, 48 + 24 * h:72 + 24 * h]), T.xlo[:, a:b], OP.subtract,
@@ -469,20 +479,30 @@ def rank_program(g, core, T, topo):
             init = 0.0 if h == 0 else T.Mx[:, a - 1:a]
             op("v", lambda: vec.tensor_tensor_scan(T.Mx[:, a:b], T["p%d" % (6 + h)][:, 0:384], T.ad[:, a:b], init, OP.mult, OP.max),
                ["#p%d" % (6 + h)] + ck("ad", a, b) + ck("Mx", 0, a), ck("Mx", a, b))
+            if h == 0:
+                tt(T.w2[:, :], T.w1[:, :], T.nW[:, :], OP.mult, ["w1", "nW"], ["w2"])
+                tt(T.w3[:, :], T.eW[:, :], T.nW[:, :], OP.mult, ["eW", "nW"], ["w3"])
+                ts(T.Le[:, :], T.w2[:, :], 768.0, None, OP.add, None, ["w2"], ["Le"])
+        sa(T.Gh[:, 1184:V], T.Z[:, :].indirect(T.Lq[:, 74:96]), AF.Identity, ck("Z") + ["Lq"], ck("Gh", 1184, V))
+        wrap("p5", 0, WU, "Gh", 0, V, 16, 0, ck("Gh"))
 
-        def agree(out, lst):
-            wk = ck("Mx", 0, 784)
-            ts(T[out][:, 0:768], T.Mx[:, :].indirect(T[lst][:, 0:48]), T.thf[:, 0:1], 0.5, OP.is_le, OP.subtract,
-               wk + [lst, "thf"], ck(out, 0, 768))
-            sa(T[out][:, 768:V], T.Mx[:, :].indirect(T[lst][:, 48:96]), AF.Sign, wk + [lst, "thb"], ck(out, 768, V),
+        def agree_v(out, lst, a, b):
+            ts(T[out][:, a:b], T.Mx[:, :].indirect(T[lst][:, a // 16:b // 16]), T.thf[:, 0:1], 0.5, OP.is_le, OP.subtract,
+               ck("Mx", 0, 784) + [lst, "thf"], ck(out, a, b))
+
+        def agree_s(out, lst, a, b):
+            sa(T[out][:, a:b], T.Mx[:, :].indirect(T[lst][:, a // 16:b // 16]), AF.Sign, ck("Mx", 0, 784) + [lst, "thb"], ck(out, a, b),
                bias=T.thb[:, 0:1], scale=-1.0)
 
-        agree("Ga", "Le")
+        agree_v("Ga", "Le", 0, 800)
+        agree_s("Ga", "Le", 800, V)
         wrap("p1", 0, WH, "Ga", 0, V, 16, 0, ck("Ga"))
+        wrap("p3", 0, WS, "Gh", 0, V, 16, 0, ck("Gh"))
         wrap("p2", 0, WA, "Ga", 0, V, 16, 0, ck("Ga"))
+        ts(T.Lf[:, :], T.w3[:, :], 768.0, None, OP.add, None, ["w3"], ["Lf"])
         tt(T.w4[:, :], T.p5[:, 0:W], T.uW[:, :], OP.subtract, ["#p5", "uW"], ["w4"])
-        agree("Gb", "Lf")
-        wrap("p0", 0, WA, "Gb", 0, V, 16, 0, ck("Gb"))
+        agree_v("Gb", "Lf", 0, 288)
+        agree_s("Gb", "Lf", 608, V)
         ts(T.w5[:, :], T.p1[:, 0:W], 0.0, None, OP.is_ge, None, ["#p1"], ["w5"])
         tt(T.w2[:, :], T.sW[:, :], T[tW][:, :], OP.subtract, ["sW", tW], ["w2"])
         tt(T.w6[:, :], T.w5[:, :], T.w4[:, :], OP.mult, ["w5", "w4"], ["w6"])
@@ -494,6 +514,8 @@ def rank_program(g, core, T, topo):
             send(T.hs[:], "hs", "ul1", "aH0", 1)
         else:
             send(T.hf[:], "hf", "yl", "aH1", 1)
+        agree_v("Gb", "Lf", 288, 608)
+        wrap("p0", 0, WA, "Gb", 0, V, 16, 0, ck("Gb"))
         ts(T.w8[:, :], T.p2[:, 0:W], 0.0, None, OP.is_ge, None, ["#p2"], ["w8"])
         ts(T.w9[:, :], T.p0[:, 0:W], 0.0, None, OP.is_ge, None, ["#p0"], ["w9"])
         tt(T.w1[:, :], T.p3[:, 0:W], T.w7[:, :], OP.subtract, ["#p3", "w7"], ["w1"])

@@ -3,14 +3,19 @@ from concourse.mybir import dt, AluOpType as OP, AxisListType, ActivationFunctio
 
 V = 1536
 W = V // 16
-NCH = 3
+NCH = 4
 CH = V // NCH
 CW = CH // 16
-GCONV = 288
-VSH = 288
+GCONV = 160
 NSTEP = 11
 BIG = 4096.0
+LQ = 4096.0
 M1 = 1.5 * 2.0 ** 23
+ZW = 4624
+ODD = 1544.0
+OPT = {"chunks": ((0, 256, 512), (512, 768, 1024), (1024, 1280, V)), "split": True, "copies": {(0, 0): (1,), (1, 0): (2,), (2, 1): (0,)},
+       "x0": 256, "scatter": (0, 384, V), "half": (384, 640, 928, 1344), "pairs": ((0, 288), (288, 512), (512, 768)),
+       "mirror": 704}
 
 
 def _f(n):
@@ -29,73 +34,67 @@ def _i(n):
     return ("sbuf", [128, n], "int32")
 
 
+WC, WS, WU, WA, WH, WL, WP = 0, 160, 320, 480, 640, 800, 960
+MP, MS, MU, FP, FA, IB, SA, SB, CB = 1120, 1248, 1376, 1504, 1632, 1760, 1856, 1880, 2208
+IF, IS, NI, ON, TR, SK, KA, KB = 0, 128, 224, 320, 448, 544, 552, 648
+RU, RS, RP, RO, RD, RA, R1 = 0, 3, 5, 8, 10, 11, 13
+
 SCRATCH = {
     "X0": _f(V), "X1": _f(V), "Y": _f(V), "Al": _f(V), "Be": _f(V), "Tt": _f(V), "Iw": _f(V), "Ic": _f(V),
-    "Xb": _b(V), "Xb0": _b(V), "Ub": _b(V), "R": _b(V), "Gl": _b(V), "Gs": _b(V), "Z": _b(V), "Gh": _b(V),
-    "Ga": _b(V), "Gb": _b(V), "xin": _b(V), "xlo": _b(768), "df": _b(768), "ad": _b(768), "Mx": _b(784),
-    "D": ("sbuf", [128, 8, 16, 16], "bfloat16"),
+    "Xb": _b(V), "Xb0": _b(V), "Ub": _b(V), "Pb": _b(V), "St": _b(V), "R": _b(V), "Gl": _b(V), "Gs": _b(V), "Gh": _b(V),
+    "Z": _b(ZW), "Ga": _b(V), "Gb": _b(V), "xin": _b(V), "xlo": _b(768), "df": _b(768), "ad": _b(768), "Mx": _b(784),
+    "X9": ("sbuf", [128, 24, 16, 4], "bfloat16"), "D": ("sbuf", [128, 8, 16, 16], "bfloat16"), "zb": _b(512),
     "ti": _i(W), "ui": _i(W), "thi": _i(4), "thf": _f(4), "thb": _f(4),
     "tl0": _u(W), "tl1": _u(W), "ul0": _u(W), "ul1": _u(W), "fl0": _u(W), "fl1": _u(W), "hs": _u(W),
     "hf": _f(W), "yl": _f(W), "tW0": _f(W), "tW1": _f(W), "tW2": _f(W),
-    "Lc": _u(W), "Ls": _u(W), "Ll": _u(W), "Lp": _u(W), "Lq": _u(W), "Le": _u(W), "Lf": _u(W), "Lo": _u(W),
-    "sW": _f(W), "uW": _f(W), "nW": _f(W), "eW": _f(W), "w1": _f(W), "w2": _f(W), "w3": _f(W), "w4": _f(W),
-    "w5": _f(W), "w6": _f(W), "w7": _f(W), "w8": _f(W), "w9": _f(W), "vW": _f(W),
-    "pi": _i(16), "pm": _i(16), "col": _f(16), "yb": _f(16), "ia": _f(8), "ib": _f(256), "A1": _f(8), "A2": _f(8),
-    "B1": _f(256), "B2": _f(256),
-    "cb": _b(1408), "cf": _f(512), "v2": _f(128), "rst": _f(128),
-    "D0": _f(128), "oi": _i(128), "pr": _i(128), "wv": _f(128), "E": _f(128), "Sc": _f(128), "rD": _f(128),
-    "dm": _f(128), "oo": _f(128), "ne": _f(128), "R0": _f(128), "Rc": _f(128), "dA": _f(128), "dB": _f(128),
-    "dC": _f(128), "d2": _f(128), "m1": _f(128), "Y1": _f(128), "Q1": _f(128), "Q2": _f(128), "Q3": _f(128),
-    "Q4": _f(128), "Q5": _f(128), "hi": _f(128), "e1": _f(128), "e2": _f(128), "nU": _f(128),
+    "Lc": _u(W), "Ld": _u(W), "Ll": _u(W), "Lp": _u(W), "Lq": _u(W), "Le": _u(W), "Lf": _u(W), "Lo": _u(W),
+    "sW": _f(W), "nW": _f(W), "w2": _f(W), "w3": _f(W), "w5": _f(W), "w8": _f(W), "vW": _f(W),
+    "hD": _f(2 * W), "hF": _f(2 * W), "hO": _f(2 * W), "tD": _f(2 * W), "tF": _f(2 * W), "tO": _f(2 * W),
+    "pi": _i(16), "pm": _i(16), "col": _f(16), "yb": _f(16), "ia": _f(16), "ib": _f(W), "A1": _f(16), "A2": _f(16),
+    "cb": _b(CB), "cf": _f(776), "rst": _f(128), "QE": _f(256),
+    "oi": _i(128), "pr": _i(128), "gg": _f(128), "Sc": _f(128), "rD": _f(128), "dd": _f(128), "q2": _f(128),
+    "zz": _f(128), "bb": _f(128), "Aq": _f(128), "mm": _f(128), "sg": _f(128), "oo": _f(128),
 }
 for _k in range(8):
     SCRATCH["p%d" % _k] = ("psum", [128, 512], "float32")
 
-SEMAPHORES = ["sv", "ss", "sg", "sp", "ldt", "ldu", "ldx", "ldh", "st0", "st1", "sent", "aT0", "aT1", "aH0", "aH1"]
+SEMAPHORES = ["sv", "ss", "sg", "sp", "ldt", "ldu", "ldx", "ldh", "zc", "zz", "st0", "st1", "sent", "aT0", "aT1", "aH0", "aH1"]
 
-WC, WS, WB, WU, WA, WH, FB, IB, SD0, SD3, ST = 0, 160, 320, 480, 640, 800, 960, 1088, 1216, 1232, 1248
-IF, IS, ON, TR, SK = 0, 128, 224, 320, 416
+SENDS = (("aT0", "fl0", -1), ("aH0", "ul1", 1), ("aT1", "fl1", -1), ("aH1", "yl", 1))
 
 
-def relay_of(T, topo, core):
+def relay_of(T, topo, src, dst):
     n = len(T.cores)
-    need = []
-    for r, c in enumerate(T.cores):
-        if c in topo.cores_of(core):
-            need += [d for d in (T.cores[(r - 1) % n], T.cores[(r + 1) % n]) if not topo.may_write(c, d)]
-    ok = [c for c in topo.cores_of(core) if c not in T.cores and all(topo.may_write(c, d) for d in need)]
-    return ok[0] if need else None
+    ok = [c for c in topo.cores_of(src) if c not in T.cores and topo.may_write(c, dst)]
+    far = [c for r, c in enumerate(T.cores) if c in topo.cores_of(src) and not topo.may_write(c, T.cores[(r + 1) % n])] + [src]
+    return sorted(ok, key=lambda c: topo.die(c) != topo.die(far[0]))[0]
 
 
-def emask(topo, src, dst, far):
-    n = len(topo.engines(src, dst)) if far is None else len(topo.engines(far[0], far[1]))
-    n = min(n, 8)
-    return sum(1 << e for e in topo.engines(src, dst)[:n]), n
+def emask(topo, src, dst):
+    e = topo.engines(src, dst)[:8]
+    return sum(1 << x for x in e), len(e)
 
 
 def relay_program(g, core, T, topo):
     n = len(T.cores)
-    jobs = []
-    for name, buf, step in (("aT0", "fl0", -1), ("aH0", "ul1", 1), ("aT1", "fl1", -1), ("aH1", "yl", 1)):
+    total = 0
+    for name, buf, step in SENDS:
         for r, c in enumerate(T.cores):
             d = T.cores[(r + step) % n]
-            if c in topo.cores_of(core) and not topo.may_write(c, d):
-                jobs.append((name, buf, c, d))
-    total = 0
-    for name, buf, c, d in jobs:
-        g.wait_ge(T.sem[name], emask(topo, c, core, None)[1])
-        m, k = emask(topo, core, d, None)
-        rid, pid = topo.addr(d, core)
-        g.remote_dma(T[buf][:], T[buf][:], T.sem[name], T.sem.sent, pid, rid, m)
-        total += k
-    g.wait_ge(T.sem.sent, total)
+            if not topo.may_write(c, d) and relay_of(T, topo, c, d) == core:
+                g.wait_ge(T.sem[name], emask(topo, c, core)[1])
+                m, k = emask(topo, core, d)
+                rid, pid = topo.addr(d, core)
+                g.remote_dma(T[buf][:], T[buf][:], T.sem[name], T.sem.sent, pid, rid, m)
+                total += k
+    if total:
+        g.wait_ge(T.sem.sent, total)
 
 
 def rank_program(g, core, T, topo):
     rank = T.rank_of(core)
     if rank is None:
-        if any(c in T.cores for c in topo.cores_of(core)) and relay_of(T, topo, core) == core:
-            relay_program(g, core, T, topo)
+        relay_program(g, core, T, topo)
         return
     n = len(T.cores)
     Q = {"v": g.vector, "s": g.scalar, "g": g, "p": g.tensor, "y": g.sync}
@@ -152,27 +151,29 @@ def rank_program(g, core, T, topo):
             cnt[s] = cnt.get(s, 0) + 1
         mark((s, cnt[s]), q, rd, wr)
 
-    def dma(q, out, in_, sem, rd, wr, **kw):
+    def dma(q, pairs, sem, rd, wr, **kw):
         deps(q, rd, wr)
-        Q[q].dma_start(out, in_, **kw).then_inc(T.sem[sem], 16)
-        cnt[sem] = 16
-        mark((sem, 16), q, rd, wr)
+        for out, in_ in pairs:
+            Q[q].dma_start(out, in_, **kw).then_inc(T.sem[sem], 16)
+        cnt[sem] = 16 * len(pairs)
+        mark((sem, cnt[sem]), q, rd, wr)
 
-    def send(src, skey, buf, sem, step):
+    def send(src, skey, which):
+        sem, buf, step = SENDS[which]
         d = T.cores[(rank + step) % n]
         if not topo.may_write(core, d):
-            d = relay_of(T, topo, core)
+            d = relay_of(T, topo, core, d)
         deps("g", [skey], [])
-        m, k = emask(topo, core, d, None)
+        m, k = emask(topo, core, d)
         rid, pid = topo.addr(d, core)
         g.remote_dma(T[buf][:], src, T.sem[sem], T.sem.sent, pid, rid, m)
         cnt["sent"] = cnt.get("sent", 0) + k
 
-    for sem, buf, step in (("aT0", "fl0", 1), ("aT1", "fl1", 1), ("aH0", "ul1", -1), ("aH1", "yl", -1)):
-        c = T.cores[(rank + step) % n]
+    for sem, buf, step in SENDS:
+        c = T.cores[(rank - step) % n]
         if not topo.may_write(c, core):
-            c = relay_of(T, topo, c)
-        k = emask(topo, c, core, None)[1]
+            c = relay_of(T, topo, c, core)
+        k = emask(topo, c, core)[1]
         cnt[sem] = k
         mark((sem, k), None, [], [buf])
 
@@ -190,41 +191,46 @@ def rank_program(g, core, T, topo):
     def cp(out, a, rd, wr):
         op("v", lambda: vec.tensor_copy(out, a), rd, wr)
 
+    def fill(out, c, wr):
+        op("v", lambda: vec.memset(out, c), [], wr)
+
     def sa(out, a, func, rd, wr, bias=0.0, scale=1.0):
         op("s", lambda: act.activation(out, a, func, bias=bias, scale=scale), rd, wr)
+
+    def mm(calls, rd, bank):
+        op("p", lambda: [pe.matmul(*c) for c in calls], rd, ["#" + bank])
 
     def ck(name, a=0, b=V):
         return ["%s:%d" % (name, j) for j in range(a // 32, (b + 31) // 32)]
 
-    def gather2(out, win, wcols, lst, split, a=0, b=V):
-        m = a + split
-        wk = ck(win, 0, wcols)
-        cp(T[out][:, a:m], T[win][:, 0:wcols].indirect(T[lst][:, a // 16:m // 16]), wk + [lst], ck(out, a, m))
-        sa(T[out][:, m:b], T[win][:, 0:wcols].indirect(T[lst][:, m // 16:b // 16]), AF.Identity, wk + [lst], ck(out, m, b))
+    def gv(out, win, wcols, lst, a, b):
+        cp(T[out][:, a:b], T[win][:, 0:wcols].indirect(T[lst][:, a // 16:b // 16]), ck(win, 0, wcols) + [lst], ck(out, a, b))
 
-    def wrap(bank, c0, base, src, a, b, step, off, rd):
-        nn = (b - a) // step
+    def gs(out, win, wcols, lst, a, b):
+        sa(T[out][:, a:b], T[win][:, 0:wcols].indirect(T[lst][:, a // 16:b // 16]), AF.Identity, ck(win, 0, wcols) + [lst], ck(out, a, b))
+
+    def gather2(out, win, wcols, lst, m, a=0, b=V):
+        gv(out, win, wcols, lst, a, m)
+        gs(out, win, wcols, lst, m, b)
+
+    def wrapv(bank, c0, nn, base, view, rd):
+        mm([(T[bank][:, c0:c0 + nn], T.cb[:, base + 16 - i:base + 144 - i], view(i), i == 0, i == 15) for i in range(16)],
+           rd + ["cb%d" % base], bank)
+
+    def wrap(bank, c0, base, src, a=0, b=V, step=16, off=0):
         mul = step // 16
-        op("p", lambda: [pe.matmul(T[bank][:, c0:c0 + nn], T.cb[:, base + 16 - i:base + 144 - i],
-                                   T[src][:, a + mul * i + off:b:step], i == 0, i == 15) for i in range(16)],
-           rd + ["cb%d" % base], ["#" + bank])
+        wrapv(bank, c0, (b - a) // step, base, lambda i: T[src][:, a + mul * i + off:b:step], ck(src, a, b))
 
-    def turn(bank, c0, ncol, sel, skey, src, rd, m0=0, m1=W):
-        op("p", lambda: [pe.matmul(T[bank][m0:m1, c0 + i:c0 + 16 * ncol:16], T[src][:, 16 * m0 + i:16 * m1:16], sel, True, True)
-                         for i in range(16)], rd + [skey], ["#" + bank])
+    def turn(bank, ncol, sel, skeys, src, add=False):
+        mm([(T[bank][0:W, i:16 * ncol:16], T[src][:, i:V:16], sel, not add, not add or i == 15) for i in range(16)], ck(src) + skeys, bank)
 
     def flip(bank, c0, srcs, extra=None):
-        calls = [(T[s][0:W, :], T.cf[0:W, idc:idc + W]) for s, idc in srcs]
-        rd = [s for s, idc in srcs] + ["cfI", "cfS"]
+        calls = [(T[s][0:W, 0:128], T.cf[0:W, idc:idc + W]) for s, idc in srcs]
+        rd = [s for s, idc in srcs] + ["cf%d" % idc for s, idc in srcs]
         if extra:
             calls = [(T.cf[:, IF:IF + 128], T[extra][:, :])] + calls
-            rd.append(extra)
-        op("p", lambda: [pe.matmul(T[bank][:, c0:c0 + W], a, b, j == 0, j == len(calls) - 1) for j, (a, b) in enumerate(calls)],
-           rd, ["#" + bank])
-
-    dma("y", T.ti[:], T.t0[:], "ldt", [], ["ti"])
-    dma("s", T.ui[:], T.u0[:], "ldu", [], ["ui"])
-    dma("y", T.xin[:], T.x[:], "ldx", [], ck("xin"))
+            rd += [extra, "cf%d" % IF]
+        mm([(T[bank][:, c0:c0 + W], a, b, j == 0, j == len(calls) - 1) for j, (a, b) in enumerate(calls)], rd, bank)
 
     def iota(out, pat, base, cm, wr, flt=True):
         if flt:
@@ -232,259 +238,320 @@ def rank_program(g, core, T, topo):
         else:
             op("g", lambda: g.iota(out, pat, base, cm), [], wr)
 
-    def put(ap, pat, base, val, key, cm=1):
-        op("g", lambda: g.affine_select(ap, ap, pat, OP.not_equal, val, base, cm), [key], [key])
+    def sel(out, a, pat, cmp, val, base, cm, rd, wr):
+        op("g", lambda: g.affine_select(out, a, pat, cmp, val, base, cm), rd, wr)
 
-    iota(T.pi[:, 0:1], [[0, 1]], 0, 1, ["pi"], False)
-    iota(T.ia[:, 0:6], [[256, 6]], 0, 0, ["ia"])
-    iota(T.ib[:, :], [[1, 256]], 0, 0, ["ib"])
-    cbkeys = ["cb%d" % b for b in (WC, WS, WB, WU, WA, WH, FB, IB, SD0, SD3)] + ["st%d" % j for j in range(8)]
-    ts(T.pm[:, 0:1], T.pi[:, 0:1], 15, None, OP.bitwise_and, None, ["pi"], ["pm"])
-    iota(T.cb[:, WC:WC + 160], [[0, 160]], 0, 0, ["cb%d" % WC])
-    iota(T.cb[:, SD0:SD0 + 16], [[0, 16]], 0, 0, ["cb%d" % SD0])
-    col = lambda j: T.col[:, j:j + 1]
-    ts(col(0), T.pm[:, 0:1], 2, 2048.0, OP.is_equal, OP.mult, ["pm"], ["c0"])
-    ts(col(1), T.pm[:, 0:1], 2, 768.0, OP.is_equal, OP.mult, ["pm"], ["c1"])
-    ts(col(2), T.pm[:, 0:1], 3, None, OP.is_equal, None, ["pm"], ["c2"])
-    ts(col(3), T.pm[:, 0:1], 4, None, OP.is_equal, None, ["pm"], ["c3"])
-    ts(col(5), T.pm[:, 0:1], 0, col(0), OP.is_equal, OP.add, ["pm", "c0"], ["c5"])
-    ts(col(6), T.pm[:, 0:1], 1, col(0), OP.is_equal, OP.add, ["pm", "c0"], ["c6"])
-    ts(col(4), T.pm[:, 0:1], 2, None, OP.is_equal, None, ["pm"], ["c4"])
-    ts(T.A1[:, 0:6], T.ia[:, 0:6], col(5), col(1), OP.mult, OP.add, ["ia", "c5", "c1"], ["A1"])
-    ts(T.B1[:, :], T.ib[:, :], col(6), None, OP.mult, None, ["ib", "c6"], ["B1"])
-    sa(T.A2[:, 0:6], T.ia[:, 0:6], AF.Identity, ["ia", "c2"], ["A2"], scale=col(2))
-    sa(T.B2[:, :], T.ib[:, :], AF.Identity, ["ib", "c3"], ["B2"], scale=col(3))
-    for a in range(6):
-        k = (256 * a, 256 * a + 256)
-        sa(T.Ic[:, k[0]:k[1]], T.B2[:, :], AF.Identity, ["A2", "B2"], ck("Ic", *k), bias=T.A2[:, a:a + 1])
-        if a == 3:
-            cp(T.tl0[:], T.ti[:], ["ti"], ["tl0"])
-        ts(T.Iw[:, k[0]:k[1]], T.B1[:, :], T.A1[:, a:a + 1], None, OP.add, None, ["A1", "B1"], ck("Iw", *k))
-    cp(T.ul0[:], T.ui[:], ["ui"], ["ul0"])
-    g8 = [[-16, 8]]
-    wv = lambda b: T.cb[:, b + 16:b + 144:16]
-    put(wv(WC), g8, 0, 1.0, "cb%d" % WC)
-    put(T.cb[:, SD0:SD0 + 8], g8, 0, 1.0, "cb%d" % SD0)
-    put(wv(WC), g8, -1, 1.0, "cb%d" % WC)
-    put(T.cb[:, SD0 + 8:SD0 + 16], g8, -1, 1.0, "cb%d" % SD0)
-    send(T.tl0[:], "tl0", "fl0", "aT0", -1)
+    def put(ap, pat, base, val, key):
+        sel(ap, ap, pat, OP.not_equal, val, base, 1, [key], [key])
 
-    def consts_v():
-        iota(T.cb[:, WS:SD0], [[0, SD0 - WS]], 0, 0, cbkeys[1:8])
-        iota(T.cb[:, SD3:ST + 64], [[0, ST + 64 - SD3]], 0, 0, cbkeys[9:])
-        iota(T.cf[:, IF:ON], [[0, ON - IF]], 0, 0, ["cfI", "cfS"])
-        iota(T.cf[:, ON:ON + W], [[0, W]], 1, 0, ["cfO"])
-        iota(T.cf[:, TR:TR + W], [[0, W]], -1, 0, ["cfT"])
-        iota(T.cf[:, SK:SK + 8], [[0, 8]], 0, 0, ["cfK"])
-        iota(wv(WA), [[0, 8]], 1, 0, ["cb%d" % WA])
-        iota(T.rst[:, :], [[0, 128]], 1, 0, ["rst"])
-        iota(T.Mx[:, 768:784], [[0, 16]], 0, 0, ["Mx:24"])
-        iota(T.rst[:, 0:128:16], [[0, 8]], 0, 0, ["rst"])
-
-    def consts_g(late):
-        tabs = [[(8, -1.0), (9, -1.0)],
-                [(10, 4096.0), (11, 4096.0), (12, 1.0), (13, 1.0), (2, 1.0), (8, 1.0), (9, 1.0)],
-                [(2, 1.0), (12, 1.0), (13, 1.0)], [(2, 1.0)],
-                [(12, -1.0), (13, -1.0), (14, 1.0), (15, 1.0)], [(14, 0.5), (15, 0.5), (2, 0.5)],
-                [(14, -1.0), (15, -1.0), (2, -2.0)], [(10, 2048.0), (11, 2048.0)]]
-        jobs = [[(T.cb[:, ST + 8 * j:ST + 8 * j + 8], g8, -t, w, "st%d" % j) for t, w in tab] for j, tab in enumerate(tabs)]
-        jobs.append([(wv(WS), g8, -t, 1.0, "cb%d" % WS) for t in (3, 4)])
-        jobs.append([(T.cb[:, SD3 + 8 * (t - 3):SD3 + 8 * (t - 2)], g8, -t, 1.0, "cb%d" % SD3) for t in (3, 4)])
-        jobs.append([(wv(WB), g8, -t, 2048.0, "cb%d" % WB) for t in (10, 11)])
-        jobs.append([(T.cb[:, WU + 32:WU + 144:16], [[-16, 7]], -t, 1.0, "cb%d" % WU) for t in (5, 6)]
-                    + [(T.cb[:, WU + 16:WU + 17], [[0, 1]], -112 - t, 1.0, "cb%d" % WU) for t in (5, 6)])
-        jobs.append([(T.cb[:, FB:FB + 128], [[-16, 8], [0, 16]], -7, 1.0, "cb%d" % FB)])
-        jobs.append([(T.cb[:, IB:IB + 128], [[-1, 128]], 0, 1.0, "cb%d" % IB)])
-        jobs.append([(T.cf[:, IF:IF + 128], [[-1, 128]], 0, 1.0, "cfI")])
-        jobs.append([(T.cf[:, IS:IS + W], [[-1, W]], 0, 1.0 / 2048, "cfS")])
-        jobs.append([(T.cf[:, SK:SK + 8], g8, -2, 1.0, "cfK")])
-        jobs = jobs[:8] + jobs[10:12] if late else jobs[8:10] + jobs[12:]
+    def puts(jobs):
         while any(jobs):
             for j in jobs:
                 if j:
                     put(*j.pop(0))
-        if late:
-            dma("g", T.thi[:, 0:1], T.th[:], "ldh", [], ["thi"], allow_slow_non_contiguous=True)
-            return
-        k = "cb%d" % WA
-        op("g", lambda: g.affine_select(wv(WA), wv(WA), g8, OP.is_ge, 0.0, 0, 1), [k], [k])
-        op("g", lambda: g.affine_select(T.cf[:, TR:TR + W], T.cf[:, TR:TR + W], [[-1, W]], OP.is_gt, 0.0, 0, 1), ["cfT"], ["cfT"])
-        op("g", lambda: g.affine_select(wv(WA), wv(WA), [[16, 8]], OP.is_ge, 0.0, 15, -1), [k], [k])
-        iota(T.v2[:, :], [[0, 8], [2048, 16]], 0, 32768, ["v2"])
-        iota(T.vW[:, :], [[16, W]], 0, 0, ["vW"])
-        iota(T.Q1[:, :], [[0, 8], [1, 16]], 0, 16, ["Q1"])
-
-    def consts_s():
-        sa(T.cb[:, WH + 32:WH + 144:16], T.cb[:, WA + 16:WA + 128:16], AF.Identity, ["cb%d" % WA], ["cb%d" % WH])
-        sa(T.cb[:, WH + 16:WH + 17], T.cb[:, WA + 128:WA + 129], AF.Identity, ["cb%d" % WA], ["cb%d" % WH])
-        sa(T.D[0:W, :, 0, :], T.Q1[0:W, :], AF.Identity, ["Q1"], ["D0_"])
-
-    def consts_late(part):
-        if part:
-            cp(T.thf[:, 0:1], T.thi[:, 0:1], ["thi"], ["thf"])
-            cp(T.tW0[:], T.ti[:], ["ti"], ["tW0"])
-            sa(T.thb[:, 0:1], T.thf[:, 0:1], AF.Identity, ["thf"], ["thb"], bias=0.5)
-            return
-        tt(T.D[0:W, :, 1, :], T.Q1[0:W, :], T.D[0:W, :, 0, :], OP.subtract, ["Q1", "D0_"], ["D1_"])
-        cp(col(7), T.pm[:, 0:1], ["pm"], ["c7"])
-        ts(T.vW[:, :], T.vW[:, :], col(7), None, OP.add, None, ["vW", "c7"], ["vW"])
 
     Dk = lambda *t: ["D%d_" % j for j in t]
-    U = lambda name: T[name][0:W, :]
+    Dr = lambda t: T.D[0:W, :, t, :]
+    U = lambda name: T[name][0:W, 0:128]
     P = lambda b, j: T[b][0:W, 128 * j:128 * j + 128]
+    col = lambda j: T.col[:, j:j + 1]
+    cbk = lambda b: "cb%d" % b
+    cfk = lambda b: "cf%d" % b
+    g8 = [[-16, 8]]
+    wv = lambda b: T.cb[:, b + 16:b + 144:16]
+    Eb = T.QE[0:W, 128:256]
 
-    def after(k, X, j, rnd):
-        a, b = CH * j, CH * j + CH
-        if k <= 9:
+    dma("y", [(T.ti[:], T.t0[:])], "ldt", [], ["ti"])
+    dma("s", [(T.ui[:], T.u0[:])], "ldu", [], ["ui"])
+
+    iota(T.pi[:, 0:1], [[0, 1]], 0, 1, ["pi"], False)
+    iota(T.ia[:, :], [[1, 16]], 0, 0, ["ia"])
+    iota(T.ib[:, :], [[1, W]], 0, 0, ["ib"])
+    fill(T.zb[:, :], 0.0, ["zb"])
+    ts(T.pm[:, 0:1], T.pi[:, 0:1], 15, None, OP.bitwise_and, None, ["pi"], ["pm"])
+    fill(T.cb[:, WC:WC + 160], 0.0, [cbk(WC)])
+    zeroed = [cbk(b) for b in (WS, WU, WA, WH, WL, WP, MP, MS, MU, FP, FA, IB)] + ["sa0", "sa1", "sa2", "sb0", "sb1"]
+    dma("y", [(T.cb[:, 160 + 512 * j:672 + 512 * j], T.zb[:, :]) for j in range(4)] + [(T.D[:, 2 * j:2 * j + 2], T.zb[:, :]) for j in range(4)],
+        "zc", ["zb"], zeroed + Dk(*range(16)))
+    dma("y", [(T.xin[:], T.x[:])], "ldx", [], ck("xin"))
+    pm = T.pm[:, 0:1]
+    ts(col(0), pm, 2, LQ, OP.is_equal, OP.mult, ["pm"], ["c0"])
+    ts(col(1), pm, 0, 16.0, OP.is_equal, OP.mult, ["pm"], ["c1"])
+    ts(col(2), pm, 1, None, OP.is_equal, None, ["pm"], ["c2"])
+    ts(col(3), pm, RS + 1, None, OP.is_equal, None, ["pm"], ["c3"])
+    ts(col(5), col(0), float(W), col(2), OP.mult, OP.add, ["c0", "c2"], ["c5"])
+    ts(col(6), col(0), V / LQ, None, OP.mult, None, ["c0"], ["c6"])
+    ts(col(7), col(0), col(1), None, OP.add, None, ["c0", "c1"], ["c7"])
+    ts(col(8), pm, RS, 16.0, OP.is_equal, OP.mult, ["pm"], ["c8"])
+    ts(T.A1[:, :], T.ia[:, :], col(5), col(6), OP.mult, OP.add, ["ia", "c5", "c6"], ["A1"])
+    ts(col(4), pm, 2, None, OP.is_equal, None, ["pm"], ["c4"])
+    sa(T.A2[:, :], T.ia[:, :], AF.Identity, ["ia", "c3"], ["A2"], scale=col(3))
+
+    def ident(q, name, A, c, i):
+        rd, wr = ["ib", A, "c%d" % c], ["%s_%d" % (name, i)]
+        if q == "v":
+            ts(T[name][:, i:V:16], T.ib[:, :], col(c), T[A][:, i:i + 1], OP.mult, OP.add, rd, wr)
+        else:
+            sa(T[name][:, i:V:16], T.ib[:, :], AF.Identity, rd, wr, bias=T[A][:, i:i + 1], scale=col(c))
+
+    for i in range(6):
+        ident("s", "Ic", "A2", 8, i)
+    cp(T.tl0[:], T.ti[:], ["ti"], ["tl0"])
+    for i in range(10):
+        ident("v", "Iw", "A1", 7, i)
+    for i in range(10, 16):
+        ident("s", "Iw", "A1", 7, i)
+    for i in range(6, 11):
+        ident("v", "Ic", "A2", 8, i)
+        ident("s", "Ic", "A2", 8, i + 5)
+    cp(T.ul0[:], T.ui[:], ["ui"], ["ul0"])
+    Iwk = ["Iw_%d" % i for i in range(16)]
+    Ick = ["Ic_%d" % i for i in range(16)]
+    puts([[(wv(WC), g8, -t, 1.0, cbk(WC)) for t in (0, 1)]])
+    send(T.tl0[:], "tl0", 0)
+
+    def consts_early():
+        diag = lambda b, t, to: (T.cb[:, b + to:b + 128:16], g8, -t, 1.0, cbk(b))
+        iota(T.cf[:, ON:ON + 128], [[0, 128]], 1, 0, [cfk(ON)])
+        iota(T.cf[:, SK:SK + 8], [[0, 8]], 0, 0, [cfk(SK)])
+        sel(T.cf[:, IF:IF + 128], T.cf[:, ON:ON + 128], [[-1, 128]], OP.is_equal, 0.0, 0, 1, [cfk(ON)], [cfk(IF)])
+        puts([[diag(MU, t, RU + t) for t in (0, 1)], [diag(MS, t, t) for t in (RS, RS + 1)], [diag(MP, t, RP + t) for t in (0, 1)],
+              [(wv(WS), g8, -t, 1.0, cbk(WS)) for t in (RS, RS + 1)] + [(T.cf[:, SK:SK + 8], g8, -2, 1.0, cfk(SK))],
+              [(T.cb[:, WU + 32:WU + 144:16], [[-16, 7]], -t, 1.0, cbk(WU)) for t in (RU, RU + 1)]
+              + [(T.cb[:, WU + 16:WU + 17], [[0, 1]], -112 - t, 1.0, cbk(WU)) for t in (RU, RU + 1)]])
+        iota(T.cf[0:2, KA:KA + W], [[int(LQ), W]], 0, 0, [cfk(KA)])
+        iota(T.cf[0:2, KB:KB + 128], [[0, 8], [-1, 16]], 0, 0, [cfk(KB)])
+        sel(T.cf[0:2, KA:KA + W], T.cf[0:2, KA:KA + W], [[0, W]], OP.is_equal, LQ * W, 0, 1, [cfk(KA)], [cfk(KA)])
+        sel(T.cf[0:2, KB:KB + 128], T.cf[0:2, KB:KB + 128], [[0, 128]], OP.is_equal, -1.0, -1, 1, [cfk(KB)], [cfk(KB)])
+        iota(T.vW[:, :], [[1, W]], 0, 0, ["vW"])
+
+    def consts_late():
+        tabs = [("sa0", SA, [(RO, 1.0), (RO + 1, 1.0)]),
+                ("sa1", SA + 8, [(RO, -1.0), (RO + 1, -1.0), (RD, -1.0), (R1, 1.0)]),
+                ("sa2", SA + 16, [(RA, 1.0), (RA + 1, 1.0), (RD, ODD), (R1, -1.0)]),
+                ("sb0", SB, [(RO, 1.0), (RO + 1, 1.0), (RD, 4096.0)]),
+                ("sb1", SB + 8, [(RD, 4096.0)])]
+        iota(T.rst[:, :], [[0, 128]], 1, 0, ["rst"])
+        iota(T.cf[:, TR:TR + W], [[0, W]], -1, 0, [cfk(TR)])
+        iota(T.rst[:, 0:128:16], [[0, 8]], 0, 0, ["rst"])
+        sel(T.cf[:, TR:TR + W], T.cf[:, TR:TR + W], [[-1, W]], OP.is_ge, 0.0, 0, 1, [cfk(TR)], [cfk(TR)])
+        iota(Dr(R1), [[0, 128]], 1, 0, Dk(R1))
+        puts([[(T.cb[:, c:c + 8], g8, -t, w, key) for t, w in tab] for key, c, tab in tabs])
+        iota(wv(WA), [[0, 8]], 1, 0, [cbk(WA)])
+        wide = [[-16, 8], [0, 16]]
+        puts([[(wv(WL), g8, -t, w, cbk(WL)) for t, w in ((RA, 0.5), (RA + 1, 0.5), (RO, 0.5), (RO + 1, 0.5), (RD, 772.0), (R1, -1.0))],
+              [(T.cb[:, FP:FP + 128], wide, -t, 256.0, cbk(FP)) for t in (0, 1)] + [(wv(WP), g8, -t, 1.0, cbk(WP)) for t in (RP, RP + 1)],
+              [(T.cb[:, FA:FA + 128], wide, -t, -128.0, cbk(FA)) for t in (RA, RA + 1)]])
+        dma("g", [(T.thi[:, 0:1], T.th[:])], "ldh", [], ["thi"], allow_slow_non_contiguous=True)
+        k, h = cbk(WA), cbk(WH)
+        iota(wv(WH), [[0, 8]], 1, 0, [h])
+        sel(wv(WA), wv(WA), g8, OP.is_ge, 0.0, 0, 1, [k], [k])
+        sel(wv(WH), wv(WH), g8, OP.is_ge, 64.0, 0, 1, [h], [h])
+        iota(T.Mx[:, 768:784], [[0, 16]], 0, 0, ["Mx:24"])
+        sel(wv(WH), wv(WH), g8, OP.is_ge, 0.0, 16, 1, [h], [h])
+        sel(wv(WA), wv(WA), [[16, 8]], OP.is_ge, 0.0, 15, -1, [k], [k])
+        sel(wv(WH), wv(WH), [[16, 8]], OP.is_ge, 0.0, 15, -1, [h], [h])
+        iota(ev("hF"), [[0, W]], 0, 0, ["hF0"])
+        sel(T.cb[:, WH + 16:WH + 17], T.cb[:, WH + 16:WH + 17], [[0, 1]], OP.is_ge, 64.0, 111, -1, [h], [h])
+        iota(ev("tF"), [[0, W]], 0, 0, ["tF0"])
+
+    def consts_step(k):
+        if k < 6:
+            sa(T.Pb[:, 256 * k:256 * k + 256], T.Iw[:, 256 * k:256 * k + 256], AF.Identity, Iwk, ck("Pb", 256 * k, 256 * k + 256))
+        if k == 6:
+            sa(T.cf[:, IS:IS + W], T.cf[:, IF:IF + W], AF.Identity, [cfk(IF)], [cfk(IS)], scale=1.0 / LQ)
+            sa(T.cf[:, NI:NI + W], T.cf[:, IF:IF + W], AF.Identity, [cfk(IF)], [cfk(NI)], scale=-1.0)
+        if k == 7:
+            sa(T.cb[:, IB:IB + W], T.cf[:, IF:IF + W], AF.Identity, [cfk(IF)], [cbk(IB)])
+            sa(T.vW[:, :], T.vW[:, :], AF.Identity, ["vW", "c9"], ["vW"], bias=col(9))
+
+    def after(k, X, j):
+        a, m, b = OPT["chunks"][j]
+        if k == 9:
+            m = m // 64 * 64
+            sa(T.X9[:, m // 64:b // 64], T[X][:, m:b], AF.Identity, ck(X, m, b), ck("X9", m, b))
+            sel(T.X9[:, a // 64:m // 64], T[X][:, a:m], [[0, m - a]], OP.is_ge, 0.0, 0, 0, ck(X, a, m), ck("X9", a, m))
+            wrapv("p%d" % j, 0, (b - a) // 16, WC, lambda i: T.X9[:, a // 64:b // 64, i // 4:16:4, i % 4], ck("X9", a, b))
+        else:
             xb = "Xb0" if k == 0 else "Xb"
-            m = a + GCONV
             sa(T[xb][:, m:b], T[X][:, m:b], AF.Identity, ck(X, m, b), ck(xb, m, b))
-            if GCONV:
-                op("g", lambda: g.affine_select(T[xb][:, a:m], T[X][:, a:m], [[0, GCONV]], OP.is_ge, 0.0, 0, 0), ck(X, a, m), ck(xb, a, m))
-            wrap("p%d" % j, 0, WC, xb, a, b, 16, 0, ck(xb, a, b))
-        if k < NSTEP:
-            sa(T.Y[:, a:b], T[X][:, a:b], AF.Identity, ck(X, a, b) + ["c4", "yb"], ck("Y", a, b), bias=T.yb[:, min(k, 9):min(k, 9) + 1], scale=col(4))
+            sel(T[xb][:, a:m], T[X][:, a:m], [[0, m - a]], OP.is_ge, 0.0, 0, 0, ck(X, a, m), ck(xb, a, m))
+            wrap("p%d" % j, 0, WC, xb, a, b)
+        sa(T.Y[:, a:b], T[X][:, a:b], AF.Identity, ck(X, a, b) + ["c4", "yb"], ck("Y", a, b), bias=T.yb[:, k:k + 1], scale=col(4))
+
+    def static(c, src, b):
+        bank, a = "p%d" % (5 + b), 512 * b
+        mm([(T[bank][:, :], T.cb[:, c:c + 128], T[src][:, a:a + 512], c == MU, c == MP)], [cbk(c)] + ck(src, a, a + 512), bank)
+
+    def lcopy(j):
+        a, m, b = OPT["chunks"][j]
+        cp(T.Lc[:, a // 16:b // 16], T["p%d" % j][:, 0:(b - a) // 16], ["#p%d" % j], ["Lc%d" % j])
+
+    ev = lambda name: T[name][:, 0:2 * W:2]
+    od = lambda name: T[name][:, 1:2 * W:2]
+
+    def pick(out, flag, data, rd):
+        op("v", lambda: vec.tensor_tensor_scan(T[out][:, :], T[flag][:, :], T[data][:, :], 0.0, OP.mult, OP.add), [flag] + rd, [out])
+
+    def pieces(k, j):
+        a, m, b = OPT["chunks"][j]
+        return ((a, m), (m, b)) if OPT["split"] else ((a, b),)
 
     for rnd in range(2):
         tl, ul, fl, tW, tN = "tl%d" % rnd, "ul%d" % rnd, "fl%d" % rnd, "tW%d" % rnd, "tW%d" % (rnd + 1)
-        gather2("Tt", "Iw", V, tl, 768)
-        tt(T.Al[:, :].indirect(T[ul][:, :]), T.Tt[:, :], T.Ic[:, :], OP.add, ck("Tt") + ck("Ic") + [ul], ck("Al"))
+        cuts = OPT["scatter"]
+        cp(T.Tt[:, 0:cuts[1]], T.Iw[:, :].indirect(T[tl][:, 0:cuts[1] // 16]), Iwk + [tl], ck("Tt", 0, cuts[1]))
+        for a, b in zip(cuts[1:], cuts[2:]):
+            sa(T.Tt[:, a:b], T.Iw[:, :].indirect(T[tl][:, a // 16:b // 16]), AF.Identity, Iwk + [tl], ck("Tt", a, b))
         if rnd == 0:
-            consts_v()
-            consts_g(False)
-            for k in range(10):
-                sa(T.yb[:, k:k + 1], col(4), AF.Identity, ["c4"], ["yb"], bias=BIG, scale=-BIG - 2.0 ** k)
-        sa(T.Ub[:, :], T.Iw[:, :].indirect(T[ul][:, :]), AF.Identity, ck("Iw") + [ul], ck("Ub"))
-        turn("p6", 0, 16, T.cb[:, SD0:SD0 + 16], "cb%d" % SD0, "Ub", ck("Ub"))
-        sa(T.D[0:W, :, 5, :], P("p6", 0), AF.Identity, ["#p6"], Dk(5))
-        sa(T.D[0:W, :, 6, :], P("p6", 1), AF.Identity, ["#p6"], Dk(6))
-        gather2("Be", "Al", V, fl, 768)
-        gather2("X0", "Be", V, ul, CH // 2, 0, CH)
-        after(0, "X0", 0, rnd)
-        for j in range(1, NCH):
-            cp(T.X0[:, CH * j:CH * j + CH], T.Be[:, :].indirect(T[ul][:, CW * j:CW * j + CW]), ck("Be") + [ul], ck("X0", CH * j, CH * j + CH))
-            after(0, "X0", j, rnd)
-        for k in range(NSTEP):
-            X, Xn = ("X0", "X1") if k % 2 == 0 else ("X1", "X0")
-            for j in range(NCH):
-                a, b = CH * j, CH * j + CH
-                lk = "Lc%d" % j
-                if k == 9 or (k < 9 and j == 0):
-                    cp(T.Lc[:, CW * j:CW * j + CW], T["p%d" % j][:, 0:CW], ["#p%d" % j], [lk])
-                for c, e in ((a, a + GCONV), (a + GCONV, b)) if k <= 8 else ((a, b),):
-                    if c > a and j + 1 < NCH:
-                        cp(T.Lc[:, CW * (j + 1):CW * (j + 2)], T["p%d" % (j + 1)][:, 0:CW], ["#p%d" % (j + 1)], ["Lc%d" % (j + 1)])
-                    tt(T[Xn][:, c:e], T[X][:, :].indirect(T.Lc[:, c // 16:e // 16]), T.Y[:, c:e], OP.min,
-                       ck(X) + [lk] + ck("Y", c, e), ck(Xn, c, e))
-                after(k + 1, Xn, j, rnd)
-                if k == NSTEP - 1:
-                    turn("p3", 0, 8, T.cf[:, SK:SK + 8], "cfK", Xn, ck(Xn, a, b), CW * j, CW * j + CW)
-            if k == 8 and rnd == 0:
-                consts_s()
-                consts_g(True)
-            if k == 9:
-                wrap("p6", 0, WS, "Xb0", 0, V, 16, 0, ck("Xb0"))
-                turn("p7", 0, 16, T.cb[:, SD3:SD3 + 16], "cb%d" % SD3, "Xb0", ck("Xb0"))
-                sa(T.sW[:, :], T.p6[:, 0:W], AF.Identity, ["#p6"], ["sW"])
-                sa(T.D[0:W, :, 3, :], P("p7", 0), AF.Identity, ["#p7"], Dk(3))
-                sa(T.D[0:W, :, 4, :], P("p7", 1), AF.Identity, ["#p7"], Dk(4))
-                if rnd == 0:
-                    consts_late(0)
-        M2 = M1 * 2048
-        tt(U("D0"), P("p3", 0), U("v2"), OP.subtract, ["#p3", "v2"], ["D0"])
-        ts(U("oi"), U("D0"), 768.0, 0.0, OP.add, OP.max, ["D0"], ["oi"])
-        ts(U("rD"), U("D0"), M2, -M2, OP.add, OP.add, ["D0"], ["rD"])
-        ts(U("pr"), U("oi"), 1, None, OP.bitwise_and, None, ["oi"], ["pr"])
-        flip("p5", 0, [("rD", IS)], "vW")
-        ts(U("wv"), U("pr"), 1.0 - 2.0 ** -12, 2.0 ** -12, OP.mult, OP.add, ["pr"], ["wv"])
-        tt(U("oo"), U("oi"), U("pr"), OP.mult, ["oi", "pr"], ["oo"])
-        tt(U("E"), U("oi"), U("wv"), OP.mult, ["oi", "wv"], ["E"])
-        sa(T.D[0:W, :, 2, :], U("wv"), AF.Sign, ["wv"], Dk(2), bias=1.0, scale=-1.0)
-        sa(T.D[0:W, :, 14, :], U("oo"), AF.Identity, ["oo"], Dk(14))
-        tt(U("ne"), U("oo"), U("oi"), OP.subtract, ["oi", "oo"], ["ne"])
-        op("v", lambda: vec.tensor_tensor_scan(U("Sc"), U("rst"), U("E"), 0.0, OP.mult, OP.add), ["rst", "E"], ["Sc"])
-        op("p", lambda: [pe.matmul(P("p4", 0), T.cf[0:W, TR:TR + W], U("E"), True, False)], ["cfT", "E"], ["#p4"])
-        op("p", lambda: [pe.matmul(P("p4", 0), T.cf[0:W, ON:ON + W], U("Sc"), False, True)], ["cfO", "Sc"], ["#p4"])
-        sa(T.D[0:W, :, 12, :], U("ne"), AF.Identity, ["ne"], Dk(12))
-        tt(U("dm"), U("D0"), U("rD"), OP.subtract, ["D0", "rD"], ["dm"])
-        tt(T.D[0:W, :, 15, :], U("oo"), T.D[0:W, :, 14, :], OP.subtract, ["oo"] + Dk(14), Dk(15))
-        tt(T.D[0:W, :, 13, :], U("ne"), T.D[0:W, :, 12, :], OP.subtract, ["ne"] + Dk(12), Dk(13))
-        sa(T.D[0:W, :, 7, :], U("dm"), AF.Sign, ["dm"], Dk(7), bias=767.0)
-        ts(T.D[0:W, :, 8, :], P("p4", 0), M1 * 64, -M1 * 64, OP.add, OP.add, ["#p4"], Dk(8))
-        ts(U("R0"), P("p4", 0), M1, -M1, OP.add, OP.add, ["#p4"], ["R0"])
-        ts(U("Rc"), P("p4", 0), M1 / 32, -M1 / 32, OP.add, OP.add, ["#p4"], ["Rc"])
-        tt(T.D[0:W, :, 9, :], U("R0"), T.D[0:W, :, 8, :], OP.subtract, ["R0"] + Dk(8), Dk(9))
-        tt(T.D[0:W, :, 10, :], U("Rc"), U("R0"), OP.subtract, ["R0", "Rc"], Dk(10))
-        tt(T.D[0:W, :, 11, :], P("p4", 0), U("Rc"), OP.subtract, ["#p4", "Rc"], Dk(11))
-        cp(T.Ll[:, :], T.p5[:, 0:W], ["#p5"], ["Ll"])
-        cp(T.Ls[:, :], T.sW[:, :], ["sW"], ["Ls"])
+            ts(col(9), pm, float(W), None, OP.mult, None, ["pm"], ["c9"])
+        for a, b in zip(cuts, cuts[1:]):
+            tt(T.Al[:, :].indirect(T[ul][:, a // 16:b // 16]), T.Tt[:, a:b], T.Ic[:, a:b], OP.add, ck("Tt", a, b) + Ick + [ul], ck("Al"))
         if rnd == 0:
-            consts_late(1)
-        sa(U("dA"), U("dm"), AF.Identity, ["dm"], ["dA"], bias=768.0 + 1535.0)
-        sa(U("dB"), U("dm"), AF.Identity, ["dm"], ["dB"], bias=768.0 - 1538.0)
-        sa(U("dC"), U("dm"), AF.Identity, ["dm"], ["dC"], bias=1.0 - 1536.0, scale=-2.0)
-        sa(U("d2"), U("dm"), AF.Identity, ["dm"], ["d2"], bias=1536.0, scale=2.0)
+            consts_early()
+            dma("y", [(T.Z[:, V * j:V * j + V], T.xin[:, :]) for j in range(3)] + [(T.Z[:, 3 * V:ZW], T.xin[:, 0:ZW - 3 * V])],
+                "zz", ck("xin") + ["Al:0"], ck("Z", 0, ZW))
+            for k in range(NSTEP):
+                sa(T.yb[:, k:k + 1], col(4), AF.Identity, ["c4"], ["yb%d" % k], bias=BIG, scale=-BIG - 2.0 ** k)
+            mark((SEM["s"], cnt[SEM["s"]]), "s", [], ["yb"])
+        sa(T.Ub[:, :], T.Iw[:, :].indirect(T[ul][:, :]), AF.Identity, Iwk + [ul], ck("Ub"))
         for b in range(3):
-            op("p", lambda: [pe.matmul(T["p%d" % b][:, i:512:16], T.D[0:W, :, :, i], T.cb[0:W, IB + 32 * b:IB + 32 * b + 32], True, True)
-                             for i in range(16)], Dk(*range(16)) + ["cb%d" % IB], ["#p%d" % b])
-        sa(T.R[:, 0:512], T.p0[:, :], AF.Identity, ["#p0"], ck("R", 0, 512))
-        cp(T.R[:, 512:1024], T.p1[:, :], ["#p1"], ck("R", 512, 1024))
-        sa(T.R[:, 1024:1536], T.p2[:, :], AF.Identity, ["#p2"], ck("R", 1024, 1536))
+            static(MU, "Ub", b)
+        wrap("p3", W, WU, "Ub")
+        gather2("Be", "Al", V, fl, 768)
+        chunks, copies = OPT["chunks"], OPT["copies"]
+        for j, (a, m, b) in enumerate(chunks):
+            if j == 0:
+                gather2("X0", "Be", V, ul, OPT["x0"], a, b)
+            for e, (c, d) in enumerate(pieces(0, j)):
+                if j > 0:
+                    gv("X0", "Be", V, ul, c, d)
+                if d == b:
+                    after(0, "X0", j)
+                for i in copies.get((j, e), ()):
+                    if i <= j:
+                        lcopy(i)
+        for k in range(NSTEP - 1):
+            X, Xn = ("X0", "X1") if k % 2 == 0 else ("X1", "X0")
+            for j, (a, m, b) in enumerate(chunks):
+                for e, (c, d) in enumerate(pieces(k + 1, j)):
+                    tt(T[Xn][:, c:d], T[X][:, :].indirect(T.Lc[:, c // 16:d // 16]), T.Y[:, c:d], OP.min,
+                       ck(X) + ["Lc%d" % j] + ck("Y", c, d), ck(Xn, c, d))
+                    if k < 9 and d == b:
+                        after(k + 1, Xn, j)
+                        if j == 0 and 1 <= k <= 4:
+                            mm([(T.p3[:, 0:W], T.cb[:, WS + 16 - i:WS + 144 - i], T.Xb0[:, i:V:16], i == 0, i == 15)
+                                for i in range(4 * k - 4, 4 * k)], ck("Xb0") + [cbk(WS)], "p3")
+                    for i in copies.get((j, e), ()):
+                        if k < 9 or i > j:
+                            lcopy(i)
+            if k == 9:
+                for q in range(4):
+                    cp(T.Ld[:, 24 * q:24 * q + 24], T.p4[:, q:W:4], ["#p4"], ["Ld%d" % q])
+            if rnd == 0:
+                consts_step(k)
+            if 1 <= k <= 6:
+                static(MS if k % 2 else MP, "Xb0" if k % 2 else "Pb", (k - 1) // 2)
+            if k == 8:
+                if rnd == 0:
+                    consts_late()
+                wrapv("p4", 0, W, WC, lambda i: T.X9[:, :, i, :], ck("X9"))
+                for q in range(4):
+                    sa(T.Tt[:, 384 * q:384 * q + 384], T.X1[:, q:V:4], AF.Identity, ck("X1") + ["c4", "yb"], ck("Tt", 384 * q, 384 * q + 384),
+                       bias=T.yb[:, 10:11], scale=col(4))
+                for b in range(3):
+                    bank, a = "p%d" % (5 + b), 512 * b
+                    sa(T.St[:, a:a + 512], T[bank][:, :], AF.Identity, ["#" + bank], ck("St", a, a + 512))
+                mm([(P("p0", 0), T.cf[0:2, KA:KA + W], T.cf[0:2, KB:KB + 128], True, False)], [cfk(KA), cfk(KB)], "p0")
+                sa(T.sW[:, :], T.p3[:, 0:W], AF.Identity, ["#p3"], ["sW"])
+                sa(od("hD"), T.p3[:, W:2 * W], AF.Identity, ["#p3"], ["uW"])
+        for q in range(4):
+            a, b = 384 * q, 384 * q + 384
+            tt(T.Be[:, a:b], T.X0[:, :].indirect(T.Ld[:, 24 * q:24 * q + 24]), T.Tt[:, a:b], OP.min,
+               ck("X0") + ["Ld%d" % q] + ck("Tt", a, b), ck("Be", a, b))
+            mm([(T.p0[0:W, 4 * j + q:128:16], T.Be[:, a + j:b:4], T.cf[:, SK:SK + 8], False, q == 3 and j == 3) for j in range(4)],
+               ck("Be", a, b) + [cfk(SK)], "p0")
+        if rnd == 0:
+            cp(T.tW0[:], T.ti[:], ["ti"], ["tW0"])
+        tt(T.w2[:, :], T.sW[:, :], T[tW][:, :], OP.subtract, ["sW", tW], ["w2"])
+        D0 = P("p0", 0)
+        ts(Eb, D0, 0.0, None, OP.max, None, ["#p0"], ["E"])
+        ts(U("oi"), D0, 0.0, None, OP.max, None, ["#p0"], ["oi"])
+        op("v", lambda: vec.tensor_tensor_scan(U("Sc"), U("rst"), Eb, 0.0, OP.mult, OP.add), ["rst", "E"], ["Sc"])
+        mm([(P("p4", 0), T.cf[0:W, TR:TR + W], Eb, True, False)], [cfk(TR), "E"], "p4")
+        mm([(P("p4", 0), T.cf[0:W, ON:ON + W], U("Sc"), False, True)], [cfk(ON), "Sc"], "p4")
+        sa(Dr(RO), Eb, AF.Identity, ["E"], Dk(RO))
+        ts(U("pr"), U("oi"), 1, None, OP.bitwise_and, None, ["oi"], ["pr"])
+        ts(U("rD"), D0, M1 * LQ, -M1 * LQ, OP.add, OP.add, ["#p0"], ["rD"])
+        ts(U("gg"), U("pr"), 1.0 + 2.0 ** -13, None, OP.add, None, ["pr"], ["gg"])
+        flip("p1", 0, [("rD", IS)], "vW")
+        tt(Dr(RO + 1), D0, Dr(RO), OP.subtract, ["#p0"] + Dk(RO), Dk(RO + 1))
+        sa(Dr(RD), U("gg"), AF.Identity, ["gg"], Dk(RD), bias=-1.0 - 2.0 ** -13)
+        tt(U("zz"), P("p4", 0), U("gg"), OP.mult, ["#p4", "gg"], ["zz"])
+        tt(U("dd"), D0, U("rD"), OP.subtract, ["#p0", "rD"], ["dd"])
+        ts(P("p4", 1), U("zz"), 2 * M1, -2 * M1, OP.add, OP.add, ["zz"], ["#p4"])
+        sa(Dr(RA), U("zz"), AF.Identity, ["zz"], Dk(RA))
+        cp(T.Ll[:, :], T.p1[:, 0:W], ["#p1"], ["Ll"])
+        tt(Dr(RA + 1), P("p4", 1), Dr(RA), OP.subtract, ["#p4"] + Dk(RA), Dk(RA + 1))
+        sa(U("q2"), U("dd"), AF.Identity, ["dd"], ["q2"], bias=-1.0, scale=2.0)
+        sa(U("QE"), U("dd"), AF.Identity, ["dd"], ["QE"], bias=1.0, scale=-2.0)
+        for b, bank in enumerate(("p5", "p6", "p7", "p2")):
+            mm([(T[bank][:, W * j:W * j + W], T.D[0:W, :, :, 4 * b + j], T.cb[0:W, IB:IB + W], True, True) for j in range(4)],
+               Dk(*range(16)) + [cbk(IB)], bank)
+            if b % 2 == 0:
+                sa(T.R[:, 384 * b:384 * b + 384], T[bank][:, 0:384], AF.Identity, ["#" + bank], ck("R", 384 * b, 384 * b + 384))
+            else:
+                cp(T.R[:, 384 * b:384 * b + 384], T[bank][:, 0:384], ["#" + bank], ck("R", 384 * b, 384 * b + 384))
+        mm([(T.p1[0:W, 0:256], T.cf[0:W, IF:IF + W], T.QE[0:W, :], True, False)], [cfk(IF), "QE", "E"], "p1")
         gather2("Gl", "R", V, "Ll", 768)
-        turn("p3", 0, 32, T.cb[:, ST:ST + 32], "st0", "Gl", ck("Gl") + ["st1", "st2", "st3"])
-        turn("p4", 0, 32, T.cb[:, ST + 32:ST + 64], "st4", "Gl", ck("Gl") + ["st5", "st6", "st7"])
-        tt(U("m1"), P("p3", 2), U("dC"), OP.is_gt, ["#p3", "dC"], ["m1"])
-        tt(U("Y1"), P("p3", 1), U("dB"), OP.add, ["#p3", "dB"], ["Y1"])
-        tt(U("Q1"), P("p3", 0), U("dA"), OP.add, ["#p3", "dA"], ["Q1"])
-        tt(U("Q2"), P("p3", 2), U("m1"), OP.mult, ["#p3", "m1"], ["Q2"])
-        tt(U("Q3"), P("p3", 3), U("Y1"), OP.mult, ["#p3", "Y1"], ["Q3"])
-        flip("p5", 0, [("Q1", IF), ("Q2", IF), ("Q3", IF)])
-        tt(U("hi"), P("p4", 0), U("d2"), OP.is_lt, ["#p4", "d2"], ["hi"])
-        tt(U("Q4"), P("p4", 2), U("hi"), OP.mult, ["#p4", "hi"], ["Q4"])
-        cp(T.Lp[:, :], T.p5[:, 0:W], ["#p5"], ["Lp"])
-        cp(T.Z[:, :].indirect(T.Lp[:, :]), T.R[:, :], ck("R") + ["Lp"], ck("Z"))
-        sa(U("Q5"), P("p4", 1), AF.Identity, ["#p4"], ["Q5"])
-        sa(U("e1"), P("p4", 3), AF.Identity, ["#p4"], ["e1"])
-        sa(U("nU"), P("p3", 3), AF.Identity, ["#p3"], ["nU"])
-        flip("p0", 0, [("Q1", IF), ("Q2", IF), ("Q3", IF), ("Q4", IF), ("Q5", IF)])
-        flip("p3", 0, [("e1", IF)])
-        flip("p3", W, [("nU", IF)])
-        wrap("p6", 0, WU, "R", 0, V, 16, 0, ck("R"))
-        sa(T.Gs[:, :], T.Gl[:, :].indirect(T.Ls[:, :]), AF.Identity, ck("Gl") + ["Ls"], ck("Gs"))
-        wrap("p7", 0, WB, "Gs", 0, V, 16, 0, ck("Gs"))
-        sa(T.w1[:, :], T.p3[:, 0:W], AF.Identity, ["#p3"], ["w1"], bias=-769.0)
-        sa(T.nW[:, :], T.p3[:, W:2 * W], AF.Identity, ["#p3"], ["nW"])
-        sa(T.uW[:, :], T.p6[:, 0:W], AF.Identity, ["#p6"], ["uW"])
-        sa(T.eW[:, :], T.p7[:, 0:W], AF.Identity, ["#p7"], ["eW"], bias=-769.0)
-        wrap("p1", 0, WC, "Z", 0, V, 32, 0, ck("Z"))
-        wrap("p2", 0, WC, "Z", 0, V, 32, 1, ck("Z"))
-        for h in range(2):
-            op("p", lambda: [pe.matmul(T["p%d" % (6 + h)][:, 0:384], T.cb[:, FB:FB + 128], T.Z[:, 768 * h:768 * h + 768:2], True, True)],
-               ck("Z") + ["cb%d" % FB], ["#p%d" % (6 + h)])
-        ts(T.Lq[:, :], T.p0[:, 0:W], 0.5, None, OP.add, None, ["#p0"], ["Lq"])
-        gather2("Gh", "Z", V, "Lq", 416, 0, 832)
-        cp(T.Lo[:, 0:48], T.p1[:, 0:48], ["#p1"], ["Lo0"])
-        cp(T.Lo[:, 48:96], T.p2[:, 0:48], ["#p2"], ["Lo1"])
-        cp(T.Gh[:, 832:1184], T.Z[:, :].indirect(T.Lq[:, 52:74]), ck("Z") + ["Lq"], ck("Gh", 832, 1184))
-        for h in range(2):
-            a, b = 384 * h, 384 * h + 384
-            sa(T.xlo[:, a:b], T.xin[:, :].indirect(T.Lo[:, 24 * h:24 * h + 24]), AF.Identity, ck("xin") + ["Lo0"], ck("xlo", a, b))
-        for h in range(2):
-            a, b = 384 * h, 384 * h + 384
-            tt(T.df[:, a:b], T.xin[:, :].indirect(T.Lo[:, 48 + 24 * h:72 + 24 * h]), T.xlo[:, a:b], OP.subtract,
+        turn("p4", 24, T.cb[:, SA:SA + 24], ["sa0", "sa1", "sa2"], "Gl")
+        tt(U("bb"), P("p4", 0), U("q2"), OP.is_le, ["#p4", "q2"], ["bb"])
+        tt(U("Aq"), P("p4", 2), U("q2"), OP.add, ["#p4", "q2"], ["Aq"])
+        mm([(T.p2[:, 0:W], U("Aq"), T.cf[0:W, IF:IF + W], True, False)], ["Aq", cfk(IF)], "p2")
+        tt(U("mm"), P("p4", 1), U("bb"), OP.mult, ["#p4", "bb"], ["mm"])
+        mm([(T.p2[:, 0:W], U("mm"), T.cf[0:W, IF:IF + W], False, True)], ["mm", cfk(IF)], "p2")
+        turn("p1", 16, T.cb[:, SB:SB + 16], ["sb0", "sb1"], "Gl", True)
+        sa(U("sg"), P("p1", 0), AF.Sign, ["#p1"], ["sg"], bias=-0.5)
+        sa(U("oo"), P("p1", 1), AF.Relu, ["#p1"], ["oo"], bias=-4096.0)
+        cp(T.Lp[:, :], T.p2[:, 0:W], ["#p2"], ["Lp"])
+        tt(T.Z[:, :].indirect(T.Lp[:, :]), T.Gl[:, :], T.St[:, :], OP.add, ck("Gl") + ck("St") + ["Lp"], ck("Z", 0, ZW))
+        sa(T.Gs[:, :], T.Gl[:, :].indirect(T[tl][:, :]), AF.Identity, ck("Gl") + [tl], ck("Gs"))
+        flip("p3", 0, [("Aq", IF), ("mm", IF), ("sg", IF), ("oo", NI)])
+        wrap("p4", 0, WL, "Gl")
+        for bank, a, b in (("p6", 0, 512), ("p7", 512, 768)):
+            mm([(T[bank][:, 0:b - a], T.cb[:, FP:FP + 128], T.Pb[:, a:b], True, False)], ck("Pb") + [cbk(FP)], bank)
+        wrap("p5", 0, WL, "Gs")
+        sa(T.nW[:, :], T.p4[:, 0:W], AF.Sign, ["#p4"], ["nW"], bias=768.0, scale=-1.0)
+        sa(T.p4[:, W:2 * W], T.nW[:, :], AF.Relu, ["nW"], ["#p4"])
+        wrap("p0", 0, WP, "Z", 0, V, 32, 0)
+        wrap("p1", 0, WP, "Z", 0, V, 32, 1)
+        for bank, a, b in (("p6", 0, 512), ("p7", 512, 768)):
+            mm([(T[bank][:, 0:b - a], T.cb[:, FA:FA + 128], T.Z[:, 2 * a:2 * b:2], False, True)], ck("Z") + [cbk(FA)], bank)
+        cp(T.Lq[:, :], T.p3[:, 0:W], ["#p3"], ["Lq"])
+        ts(T.Le[:, :], T.p4[:, 0:W], 768.0, None, OP.min, None, ["#p4"], ["Le"])
+        h0, h1, h2, h3 = OPT["half"]
+        gs("Gh", "Z", ZW, "Lq", 0, h0)
+        gv("Gh", "Z", ZW, "Lq", h0, h1)
+        cp(T.Lo[:, 0:48], T.p0[:, 0:48], ["#p0"], ["Lo0"])
+        gv("Gh", "Z", ZW, "Lq", h1, h2)
+        cp(T.Lo[:, 48:96], T.p1[:, 0:48], ["#p1"], ["Lo1"])
+        gv("Gh", "Z", ZW, "Lq", h2, h3)
+
+        def low(a, b):
+            sa(T.xlo[:, a:b], T.xin[:, :].indirect(T.Lo[:, a // 16:b // 16]), AF.Identity, ck("xin") + ["Lo0"], ck("xlo", a, b))
+
+        def gap(a, b):
+            tt(T.df[:, a:b], T.xin[:, :].indirect(T.Lo[:, 48 + a // 16:48 + b // 16]), T.xlo[:, a:b], OP.subtract,
                ck("xin") + ["Lo1"] + ck("xlo", a, b), ck("df", a, b))
+
+        def size(a, b):
             sa(T.ad[:, a:b], T.df[:, a:b], AF.Abs, ck("df", a, b), ck("ad", a, b))
-        for h in range(2):
-            a, b = 384 * h, 384 * h + 384
-            init = 0.0 if h == 0 else T.Mx[:, a - 1:a]
-            op("v", lambda: vec.tensor_tensor_scan(T.Mx[:, a:b], T["p%d" % (6 + h)][:, 0:384], T.ad[:, a:b], init, OP.mult, OP.max),
-               ["#p%d" % (6 + h)] + ck("ad", a, b) + ck("Mx", 0, a), ck("Mx", a, b))
-            if h == 0:
-                tt(T.w2[:, :], T.w1[:, :], T.nW[:, :], OP.mult, ["w1", "nW"], ["w2"])
-                tt(T.w3[:, :], T.eW[:, :], T.nW[:, :], OP.mult, ["eW", "nW"], ["w3"])
-                ts(T.Le[:, :], T.w2[:, :], 768.0, None, OP.add, None, ["w2"], ["Le"])
-        sa(T.Gh[:, 1184:V], T.Z[:, :].indirect(T.Lq[:, 74:96]), AF.Identity, ck("Z") + ["Lq"], ck("Gh", 1184, V))
-        wrap("p5", 0, WU, "Gh", 0, V, 16, 0, ck("Gh"))
+
+        def scan(a, b):
+            bank = "p%d" % (6 + a // 512)
+            init = 0.0 if a == 0 else T.Mx[:, a - 1:a]
+            op("v", lambda: vec.tensor_tensor_scan(T.Mx[:, a:b], T[bank][:, a % 512:a % 512 + b - a], T.ad[:, a:b], init, OP.min, OP.max),
+               ["#" + bank] + ck("ad", a, b) + ck("Mx", 0, a), ck("Mx", a, b))
 
         def agree_v(out, lst, a, b):
             ts(T[out][:, a:b], T.Mx[:, :].indirect(T[lst][:, a // 16:b // 16]), T.thf[:, 0:1], 0.5, OP.is_le, OP.subtract,
@@ -494,39 +561,53 @@ def rank_program(g, core, T, topo):
             sa(T[out][:, a:b], T.Mx[:, :].indirect(T[lst][:, a // 16:b // 16]), AF.Sign, ck("Mx", 0, 784) + [lst, "thb"], ck(out, a, b),
                bias=T.thb[:, 0:1], scale=-1.0)
 
-        agree_v("Ga", "Le", 0, 800)
-        agree_s("Ga", "Le", 800, V)
-        wrap("p1", 0, WH, "Ga", 0, V, 16, 0, ck("Ga"))
-        wrap("p3", 0, WS, "Gh", 0, V, 16, 0, ck("Gh"))
-        wrap("p2", 0, WA, "Ga", 0, V, 16, 0, ck("Ga"))
-        ts(T.Lf[:, :], T.w3[:, :], 768.0, None, OP.add, None, ["w3"], ["Lf"])
-        tt(T.w4[:, :], T.p5[:, 0:W], T.uW[:, :], OP.subtract, ["#p5", "uW"], ["w4"])
-        agree_v("Gb", "Lf", 0, 288)
-        agree_s("Gb", "Lf", 608, V)
-        ts(T.w5[:, :], T.p1[:, 0:W], 0.0, None, OP.is_ge, None, ["#p1"], ["w5"])
-        tt(T.w2[:, :], T.sW[:, :], T[tW][:, :], OP.subtract, ["sW", tW], ["w2"])
-        tt(T.w6[:, :], T.w5[:, :], T.w4[:, :], OP.mult, ["w5", "w4"], ["w6"])
-        tt(T.w3[:, :], T.w2[:, :], T.nW[:, :], OP.mult, ["w2", "nW"], ["w3"])
-        tt(T.hf[:, :], T.w6[:, :], T.uW[:, :], OP.add, ["w6", "uW"], ["hf"])
-        tt(T.w7[:, :], T.w3[:, :], T[tW][:, :], OP.add, ["w3", tW], ["w7"])
+        c0, c1, c2 = OPT["pairs"]
+        low(*c0)
+        low(*c1)
+        low(*c2)
+        gs("Gh", "Z", ZW, "Lq", h3, V)
+        wrap("p2", 0, WU, "Gh")
+        wrap("p3", 0, WS, "Gh")
+        gap(*c0)
+        gap(*c1)
+        size(*c0)
+        gap(*c2)
+        size(*c1)
+        size(*c2)
         if rnd == 0:
-            cp(T.hs[:, :], T.hf[:, :], ["hf"], ["hs"])
-            send(T.hs[:], "hs", "ul1", "aH0", 1)
+            cp(T.thf[:, 0:1], T.thi[:, 0:1], ["thi"], ["thf"])
+            sa(T.thb[:, 0:1], T.thf[:, 0:1], AF.Identity, ["thf"], ["thb"], bias=0.5)
+        ts(T.Lf[:, :], T.p5[:, 0:W], 768.0, None, OP.min, None, ["#p5"], ["Lf"])
+        scan(c0[0], c1[1])
+        tt(T.w3[:, :], T.p4[:, W:2 * W], T.w2[:, :], OP.mult, ["#p4", "w2"], ["w3"])
+        tt(ev("hD"), T.p2[:, 0:W], od("hD"), OP.subtract, ["#p2", "uW"], ["w4"])
+        scan(*c2)
+        tt(od("tD"), T.w3[:, :], T[tW][:, :], OP.add, ["w3", tW], ["w7"])
+        agree_v("Ga", "Le", 0, 768)
+        agree_s("Ga", "Le", 768, V)
+        wrap("p0", 0, WH, "Ga")
+        agree_s("Gb", "Lf", OPT["mirror"], V)
+        agree_v("Gb", "Lf", 0, OPT["mirror"])
+        wrap("p1", 0, WA, "Gb")
+        ts(od("hF"), T.p0[:, 0:W], -32.0, None, OP.is_ge, None, ["#p0", "hF0"], ["hF"])
+        ts(T.w5[:, :], T.p0[:, 0:W], 64 * M1, -64 * M1, OP.add, OP.add, ["#p0"], ["w5"])
+        tt(ev("tD"), T.p3[:, 0:W], od("tD"), OP.subtract, ["#p3", "w7"], ["w1"])
+        pick("hO", "hF", "hD", ["w4", "uW"])
+        tt(T.w8[:, :], T.p0[:, 0:W], T.w5[:, :], OP.is_ge, ["#p0", "w5"], ["w8"])
+        hs = "hs" if rnd == 0 else "hf"
+        cp(T[hs][:, :], od("hO"), ["hO"], [hs])
+        send(T[hs][:], hs, 1 + 2 * rnd)
+        ts(T.p1[:, W:2 * W], T.p1[:, 0:W], 0.0, None, OP.is_ge, None, ["#p1"], ["#p1"])
+        tt(od("tF"), T.p1[:, W:2 * W], T.w8[:, :], OP.not_equal, ["#p1", "w8", "tF0"], ["tF"])
+        pick("tO", "tF", "tD", ["w1", "w7"])
+        if rnd == 0:
+            cp(T.tl1[:, :], od("tO"), ["tO"], ["tl1"])
+            send(T.tl1[:], "tl1", 2)
+            sa(T[tN][:, :], od("tO"), AF.Identity, ["tO"], [tN])
         else:
-            send(T.hf[:], "hf", "yl", "aH1", 1)
-        agree_v("Gb", "Lf", 288, 608)
-        wrap("p0", 0, WA, "Gb", 0, V, 16, 0, ck("Gb"))
-        ts(T.w8[:, :], T.p2[:, 0:W], 0.0, None, OP.is_ge, None, ["#p2"], ["w8"])
-        ts(T.w9[:, :], T.p0[:, 0:W], 0.0, None, OP.is_ge, None, ["#p0"], ["w9"])
-        tt(T.w1[:, :], T.p3[:, 0:W], T.w7[:, :], OP.subtract, ["#p3", "w7"], ["w1"])
-        tt(T.w5[:, :], T.w8[:, :], T.w9[:, :], OP.not_equal, ["w8", "w9"], ["w5"])
-        tt(T.w6[:, :], T.w5[:, :], T.w1[:, :], OP.mult, ["w5", "w1"], ["w6"])
-        tt(T[tN][:, :], T.w6[:, :], T.w7[:, :], OP.add, ["w6", "w7"], [tN])
-        if rnd == 0:
-            cp(T.tl1[:, :], T[tN][:, :], [tN], ["tl1"])
-            send(T.tl1[:], "tl1", "fl1", "aT1", -1)
-    dma("y", T.yt[:], T.tW2[:], "st0", ["tW2"], [])
-    dma("s", T.yu[:], T.yl[:], "st1", ["yl"], [])
+            cp(T[tN][:, :], od("tO"), ["tO"], [tN])
+    dma("y", [(T.yt[:], T.tW2[:])], "st0", ["tW2"], [])
+    dma("s", [(T.yu[:], T.yl[:])], "st1", ["yl"], [])
     for s, c in cnt.items():
         if clock["g"].get(s, 0) < c:
             g.wait_ge(T.sem[s], c)

from concourse.bass import DstId, RemoteDMATransfer
from concourse.mybir import dt, AluOpType as OP, AxisListType, ActivationFunctionType as AF

V = 1536
W = V // 16
NCH = 4
CH = V // NCH
CW = CH // 16
GCONV = 160
NSTEP = 11
BIG = 4096.0
LQ = 4096.0
M1 = 1.5 * 2.0 ** 23
ZW = 4624
ODD = 1544.0
OPT = {"chunks": ((0, 256, 512), (512, 768, 1024), (1024, 1280, V)), "split": True, "copies": {(0, 0): (1,), (1, 0): (2,), (2, 1): (0,)},
       "x0": 256, "scatter": (0, 384, V), "half": (384, 640, 928, 1344), "pairs": ((0, 288), (288, 512), (512, 768)),
       "mirror": 704}


def _f(n):
    return ("sbuf", [128, n], "float32")


def _b(n):
    return ("sbuf", [128, n], "bfloat16")


def _u(n):
    return ("sbuf", [128, n], "uint16")


def _i(n):
    return ("sbuf", [128, n], "int32")


WC, WS, WU, WA, WH, WL, WP = 0, 160, 320, 480, 640, 800, 960
MP, MS, MU, FP, FA, IB, SA, SB, CB = 1120, 1248, 1376, 1504, 1632, 1760, 1856, 1880, 2208
IF, IS, NI, ON, TR, SK, KA, KB = 0, 128, 224, 320, 448, 544, 552, 648
RU, RS, RP, RO, RD, RA, R1 = 0, 3, 5, 8, 10, 11, 13

SCRATCH = {
    "X0": _f(V), "X1": _f(V), "Y": _f(V), "Al": _f(V), "Be": _f(V), "Tt": _f(V), "Iw": _f(V), "Ic": _f(V),
    "Xb": _b(V), "Xb0": _b(V), "Ub": _b(V), "Pb": _b(V), "St": _b(V), "R": _b(V), "Gl": _b(V), "Gs": _b(V), "Gh": _b(V),
    "Z": _b(ZW), "Ga": _b(V), "Gb": _b(V), "xin": _b(V), "xlo": _b(768), "df": _b(768), "ad": _b(768), "Mx": _b(784),
    "X9": ("sbuf", [128, 24, 16, 4], "bfloat16"), "D": ("sbuf", [128, 8, 16, 16], "bfloat16"), "zb": _b(512),
    "ti": _i(W), "ui": _i(W), "thi": _i(4), "thf": _f(4), "thb": _f(4),
    "tl0": _u(W), "tl1": _u(W), "ul0": _u(W), "ul1": _u(W), "fl0": _u(W), "fl1": _u(W), "hs": _u(W),
    "hf": _f(W), "yl": _f(W), "tW0": _f(W), "tW1": _f(W), "tW2": _f(W),
    "Lc": _u(W), "Ld": _u(W), "Ll": _u(W), "Lp": _u(W), "Lq": _u(W), "Le": _u(W), "Lf": _u(W), "Lo": _u(W),
    "sW": _f(W), "nW": _f(W), "w2": _f(W), "w3": _f(W), "w5": _f(W), "w8": _f(W), "vW": _f(W),
    "hD": _f(2 * W), "hF": _f(2 * W), "hO": _f(2 * W), "tD": _f(2 * W), "tF": _f(2 * W), "tO": _f(2 * W),
    "pi": _i(16), "pm": _i(16), "col": _f(16), "yb": _f(16), "ia": _f(16), "ib": _f(W), "A1": _f(16), "A2": _f(16),
    "cb": _b(CB), "cf": _f(776), "rst": _f(128), "QE": _f(256),
    "oi": _i(128), "pr": _i(128), "gg": _f(128), "Sc": _f(128), "rD": _f(128), "dd": _f(128), "q2": _f(128),
    "zz": _f(128), "bb": _f(128), "Aq": _f(128), "mm": _f(128), "sg": _f(128), "oo": _f(128),
}
for _k in range(8):
    SCRATCH["p%d" % _k] = ("psum", [128, 512], "float32")

SEMAPHORES = ["sv", "ss", "sg", "sp", "ldt", "ldu", "ldx", "ldh", "zc", "zz", "st0", "st1", "sent", "aT0", "aT1", "aH0", "aH1"]

SENDS = (("aT0", "fl0", -1), ("aH0", "ul1", 1), ("aT1", "fl1", -1), ("aH1", "yl", 1))


def relay_of(T, topo, src, dst):
    n = len(T.cores)
    ok = [c for c in topo.cores_of(src) if c not in T.cores and topo.may_write(c, dst)]
    far = [c for r, c in enumerate(T.cores) if c in topo.cores_of(src) and not topo.may_write(c, T.cores[(r + 1) % n])] + [src]
    return sorted(ok, key=lambda c: topo.die(c) != topo.die(far[0]))[0]


def emask(topo, src, dst):
    e = topo.engines(src, dst)[:8]
    return sum(1 << x for x in e), len(e)


def relay_program(g, core, T, topo):
    n = len(T.cores)
    total = 0
    for name, buf, step in SENDS:
        for r, c in enumerate(T.cores):
            d = T.cores[(r + step) % n]
            if not topo.may_write(c, d) and relay_of(T, topo, c, d) == core:
                g.wait_ge(T.sem[name], emask(topo, c, core)[1])
                m, k = emask(topo, core, d)
                rid, pid = topo.addr(d, core)
                g.remote_dma(T[buf][:], T[buf][:], T.sem[name], T.sem.sent, pid, rid, m)
                total += k
    if total:
        g.wait_ge(T.sem.sent, total)


def rank_program(g, core, T, topo):
    rank = T.rank_of(core)
    if rank is None:
        relay_program(g, core, T, topo)
        return
    n = len(T.cores)
    Q = {"v": g.vector, "s": g.scalar, "g": g, "p": g.tensor, "y": g.sync}
    SEM = {"v": "sv", "s": "ss", "g": "sg", "p": "sp"}
    cnt = {}
    clock = {q: {} for q in Q}
    tokclock = {}
    writer = {}
    readers = {}

    def need(q, tok):
        s, c = tok
        if clock[q].get(s, 0) >= c:
            return
        Q[q].wait_ge(T.sem[s], c)
        for k, x in tokclock[tok].items():
            if clock[q].get(k, 0) < x:
                clock[q][k] = x

    def mark(tok, q, rd, wr):
        ck = dict(clock[q]) if q else {}
        ck[tok[0]] = tok[1]
        tokclock[tok] = ck
        for k in rd:
            readers.setdefault(k, []).append(tok)
        for k in wr:
            writer[k] = tok
            readers[k] = []

    def deps(q, rd, wr):
        own = SEM.get(q)
        ts = []
        for k in rd:
            if k in writer:
                ts.append(writer[k])
            if k[0] == "#":
                ts += [t for t in readers.get(k, []) if t[0] != own]
        for k in wr:
            if k in writer and not (q == "p" and writer[k][0] == own):
                ts.append(writer[k])
            ts += [t for t in readers.get(k, []) if not (q == "p" and t[0] == own)]
        best = {}
        for s, c in ts:
            best[s] = max(best.get(s, 0), c)
        for s, c in sorted(best.items(), key=lambda z: z[0] == own):
            need(q, (s, c))

    def op(q, fn, rd, wr):
        deps(q, rd, wr)
        r = fn()
        s = SEM[q]
        for x in (r if isinstance(r, list) else [r]):
            x.then_inc(T.sem[s], 1)
            cnt[s] = cnt.get(s, 0) + 1
        mark((s, cnt[s]), q, rd, wr)

    def dma(q, pairs, sem, rd, wr, **kw):
        deps(q, rd, wr)
        for out, in_ in pairs:
            Q[q].dma_start(out, in_, **kw).then_inc(T.sem[sem], 16)
        cnt[sem] = 16 * len(pairs)
        mark((sem, cnt[sem]), q, rd, wr)

    def send(src, skey, which):
        sem, buf, step = SENDS[which]
        d = T.cores[(rank + step) % n]
        if not topo.may_write(core, d):
            d = relay_of(T, topo, core, d)
        deps("g", [skey], [])
        m, k = emask(topo, core, d)
        rid, pid = topo.addr(d, core)
        g.remote_dma(T[buf][:], src, T.sem[sem], T.sem.sent, pid, rid, m)
        cnt["sent"] = cnt.get("sent", 0) + k

    for sem, buf, step in SENDS:
        c = T.cores[(rank - step) % n]
        if not topo.may_write(c, core):
            c = relay_of(T, topo, c, core)
        k = emask(topo, c, core)[1]
        cnt[sem] = k
        mark((sem, k), None, [], [buf])

    vec, act, pe = g.vector, g.scalar, g.tensor

    def ts(out, in0, s1, s2, o0, o1, rd, wr):
        if o1 is None:
            op("v", lambda: vec.tensor_scalar(out, in0, s1, None, o0), rd, wr)
        else:
            op("v", lambda: vec.tensor_scalar(out, in0, s1, s2, o0, o1), rd, wr)

    def tt(out, a, b, o, rd, wr):
        op("v", lambda: vec.tensor_tensor(out, a, b, o), rd, wr)

    def cp(out, a, rd, wr):
        op("v", lambda: vec.tensor_copy(out, a), rd, wr)

    def fill(out, c, wr):
        op("v", lambda: vec.memset(out, c), [], wr)

    def sa(out, a, func, rd, wr, bias=0.0, scale=1.0):
        op("s", lambda: act.activation(out, a, func, bias=bias, scale=scale), rd, wr)

    def mm(calls, rd, bank):
        op("p", lambda: [pe.matmul(*c) for c in calls], rd, ["#" + bank])

    def ck(name, a=0, b=V):
        return ["%s:%d" % (name, j) for j in range(a // 32, (b + 31) // 32)]

    def gv(out, win, wcols, lst, a, b):
        cp(T[out][:, a:b], T[win][:, 0:wcols].indirect(T[lst][:, a // 16:b // 16]), ck(win, 0, wcols) + [lst], ck(out, a, b))

    def gs(out, win, wcols, lst, a, b):
        sa(T[out][:, a:b], T[win][:, 0:wcols].indirect(T[lst][:, a // 16:b // 16]), AF.Identity, ck(win, 0, wcols) + [lst], ck(out, a, b))

    def gather2(out, win, wcols, lst, m, a=0, b=V):
        gv(out, win, wcols, lst, a, m)
        gs(out, win, wcols, lst, m, b)

    def wrapv(bank, c0, nn, base, view, rd):
        mm([(T[bank][:, c0:c0 + nn], T.cb[:, base + 16 - i:base + 144 - i], view(i), i == 0, i == 15) for i in range(16)],
           rd + ["cb%d" % base], bank)

    def wrap(bank, c0, base, src, a=0, b=V, step=16, off=0):
        mul = step // 16
        wrapv(bank, c0, (b - a) // step, base, lambda i: T[src][:, a + mul * i + off:b:step], ck(src, a, b))

    def turn(bank, ncol, sel, skeys, src, add=False):
        mm([(T[bank][0:W, i:16 * ncol:16], T[src][:, i:V:16], sel, not add, not add or i == 15) for i in range(16)], ck(src) + skeys, bank)

    def flip(bank, c0, srcs, extra=None):
        calls = [(T[s][0:W, 0:128], T.cf[0:W, idc:idc + W]) for s, idc in srcs]
        rd = [s for s, idc in srcs] + ["cf%d" % idc for s, idc in srcs]
        if extra:
            calls = [(T.cf[:, IF:IF + 128], T[extra][:, :])] + calls
            rd += [extra, "cf%d" % IF]
        mm([(T[bank][:, c0:c0 + W], a, b, j == 0, j == len(calls) - 1) for j, (a, b) in enumerate(calls)], rd, bank)

    def iota(out, pat, base, cm, wr, flt=True):
        if flt:
            op("g", lambda: g.iota(out, pat, base, cm, allow_small_or_imprecise_dtypes=True), [], wr)
        else:
            op("g", lambda: g.iota(out, pat, base, cm), [], wr)

    def sel(out, a, pat, cmp, val, base, cm, rd, wr):
        op("g", lambda: g.affine_select(out, a, pat, cmp, val, base, cm), rd, wr)

    def put(ap, pat, base, val, key):
        sel(ap, ap, pat, OP.not_equal, val, base, 1, [key], [key])

    def puts(jobs):
        while any(jobs):
            for j in jobs:
                if j:
                    put(*j.pop(0))

    Dk = lambda *t: ["D%d_" % j for j in t]
    Dr = lambda t: T.D[0:W, :, t, :]
    U = lambda name: T[name][0:W, 0:128]
    P = lambda b, j: T[b][0:W, 128 * j:128 * j + 128]
    col = lambda j: T.col[:, j:j + 1]
    cbk = lambda b: "cb%d" % b
    cfk = lambda b: "cf%d" % b
    g8 = [[-16, 8]]
    wv = lambda b: T.cb[:, b + 16:b + 144:16]
    Eb = T.QE[0:W, 128:256]

    dma("y", [(T.ti[:], T.t0[:])], "ldt", [], ["ti"])
    dma("s", [(T.ui[:], T.u0[:])], "ldu", [], ["ui"])

    iota(T.pi[:, 0:1], [[0, 1]], 0, 1, ["pi"], False)
    iota(T.ia[:, :], [[1, 16]], 0, 0, ["ia"])
    iota(T.ib[:, :], [[1, W]], 0, 0, ["ib"])
    fill(T.zb[:, :], 0.0, ["zb"])
    ts(T.pm[:, 0:1], T.pi[:, 0:1], 15, None, OP.bitwise_and, None, ["pi"], ["pm"])
    fill(T.cb[:, WC:WC + 160], 0.0, [cbk(WC)])
    zeroed = [cbk(b) for b in (WS, WU, WA, WH, WL, WP, MP, MS, MU, FP, FA, IB)] + ["sa0", "sa1", "sa2", "sb0", "sb1"]
    dma("y", [(T.cb[:, 160 + 512 * j:672 + 512 * j], T.zb[:, :]) for j in range(4)] + [(T.D[:, 2 * j:2 * j + 2], T.zb[:, :]) for j in range(4)],
        "zc", ["zb"], zeroed + Dk(*range(16)))
    dma("y", [(T.xin[:], T.x[:])], "ldx", [], ck("xin"))
    pm = T.pm[:, 0:1]
    ts(col(0), pm, 2, LQ, OP.is_equal, OP.mult, ["pm"], ["c0"])
    ts(col(1), pm, 0, 16.0, OP.is_equal, OP.mult, ["pm"], ["c1"])
    ts(col(2), pm, 1, None, OP.is_equal, None, ["pm"], ["c2"])
    ts(col(3), pm, RS + 1, None, OP.is_equal, None, ["pm"], ["c3"])
    ts(col(5), col(0), float(W), col(2), OP.mult, OP.add, ["c0", "c2"], ["c5"])
    ts(col(6), col(0), V / LQ, None, OP.mult, None, ["c0"], ["c6"])
    ts(col(7), col(0), col(1), None, OP.add, None, ["c0", "c1"], ["c7"])
    ts(col(8), pm, RS, 16.0, OP.is_equal, OP.mult, ["pm"], ["c8"])
    ts(T.A1[:, :], T.ia[:, :], col(5), col(6), OP.mult, OP.add, ["ia", "c5", "c6"], ["A1"])
    ts(col(4), pm, 2, None, OP.is_equal, None, ["pm"], ["c4"])
    sa(T.A2[:, :], T.ia[:, :], AF.Identity, ["ia", "c3"], ["A2"], scale=col(3))

    def ident(q, name, A, c, i):
        rd, wr = ["ib", A, "c%d" % c], ["%s_%d" % (name, i)]
        if q == "v":
            ts(T[name][:, i:V:16], T.ib[:, :], col(c), T[A][:, i:i + 1], OP.mult, OP.add, rd, wr)
        else:
            sa(T[name][:, i:V:16], T.ib[:, :], AF.Identity, rd, wr, bias=T[A][:, i:i + 1], scale=col(c))

    for i in range(6):
        ident("s", "Ic", "A2", 8, i)
    cp(T.tl0[:], T.ti[:], ["ti"], ["tl0"])
    for i in range(10):
        ident("v", "Iw", "A1", 7, i)
    for i in range(10, 16):
        ident("s", "Iw", "A1", 7, i)
    for i in range(6, 11):
        ident("v", "Ic", "A2", 8, i)
        ident("s", "Ic", "A2", 8, i + 5)
    cp(T.ul0[:], T.ui[:], ["ui"], ["ul0"])
    Iwk = ["Iw_%d" % i for i in range(16)]
    Ick = ["Ic_%d" % i for i in range(16)]
    puts([[(wv(WC), g8, -t, 1.0, cbk(WC)) for t in (0, 1)]])
    send(T.tl0[:], "tl0", 0)

    def consts_early():
        diag = lambda b, t, to: (T.cb[:, b + to:b + 128:16], g8, -t, 1.0, cbk(b))
        iota(T.cf[:, ON:ON + 128], [[0, 128]], 1, 0, [cfk(ON)])
        iota(T.cf[:, SK:SK + 8], [[0, 8]], 0, 0, [cfk(SK)])
        sel(T.cf[:, IF:IF + 128], T.cf[:, ON:ON + 128], [[-1, 128]], OP.is_equal, 0.0, 0, 1, [cfk(ON)], [cfk(IF)])
        puts([[diag(MU, t, RU + t) for t in (0, 1)], [diag(MS, t, t) for t in (RS, RS + 1)], [diag(MP, t, RP + t) for t in (0, 1)],
              [(wv(WS), g8, -t, 1.0, cbk(WS)) for t in (RS, RS + 1)] + [(T.cf[:, SK:SK + 8], g8, -2, 1.0, cfk(SK))],
              [(T.cb[:, WU + 32:WU + 144:16], [[-16, 7]], -t, 1.0, cbk(WU)) for t in (RU, RU + 1)]
              + [(T.cb[:, WU + 16:WU + 17], [[0, 1]], -112 - t, 1.0, cbk(WU)) for t in (RU, RU + 1)]])
        iota(T.cf[0:2, KA:KA + W], [[int(LQ), W]], 0, 0, [cfk(KA)])
        iota(T.cf[0:2, KB:KB + 128], [[0, 8], [-1, 16]], 0, 0, [cfk(KB)])
        sel(T.cf[0:2, KA:KA + W], T.cf[0:2, KA:KA + W], [[0, W]], OP.is_equal, LQ * W, 0, 1, [cfk(KA)], [cfk(KA)])
        sel(T.cf[0:2, KB:KB + 128], T.cf[0:2, KB:KB + 128], [[0, 128]], OP.is_equal, -1.0, -1, 1, [cfk(KB)], [cfk(KB)])
        iota(T.vW[:, :], [[1, W]], 0, 0, ["vW"])

    def consts_late():
        tabs = [("sa0", SA, [(RO, 1.0), (RO + 1, 1.0)]),
                ("sa1", SA + 8, [(RO, -1.0), (RO + 1, -1.0), (RD, -1.0), (R1, 1.0)]),
                ("sa2", SA + 16, [(RA, 1.0), (RA + 1, 1.0), (RD, ODD), (R1, -1.0)]),
                ("sb0", SB, [(RO, 1.0), (RO + 1, 1.0), (RD, 4096.0)]),
                ("sb1", SB + 8, [(RD, 4096.0)])]
        iota(T.rst[:, :], [[0, 128]], 1, 0, ["rst"])
        iota(T.cf[:, TR:TR + W], [[0, W]], -1, 0, [cfk(TR)])
        iota(T.rst[:, 0:128:16], [[0, 8]], 0, 0, ["rst"])
        sel(T.cf[:, TR:TR + W], T.cf[:, TR:TR + W], [[-1, W]], OP.is_ge, 0.0, 0, 1, [cfk(TR)], [cfk(TR)])
        iota(Dr(R1), [[0, 128]], 1, 0, Dk(R1))
        puts([[(T.cb[:, c:c + 8], g8, -t, w, key) for t, w in tab] for key, c, tab in tabs])
        iota(wv(WA), [[0, 8]], 1, 0, [cbk(WA)])
        wide = [[-16, 8], [0, 16]]
        puts([[(wv(WL), g8, -t, w, cbk(WL)) for t, w in ((RA, 0.5), (RA + 1, 0.5), (RO, 0.5), (RO + 1, 0.5), (RD, 772.0), (R1, -1.0))],
              [(T.cb[:, FP:FP + 128], wide, -t, 256.0, cbk(FP)) for t in (0, 1)] + [(wv(WP), g8, -t, 1.0, cbk(WP)) for t in (RP, RP + 1)],
              [(T.cb[:, FA:FA + 128], wide, -t, -128.0, cbk(FA)) for t in (RA, RA + 1)]])
        dma("g", [(T.thi[:, 0:1], T.th[:])], "ldh", [], ["thi"], allow_slow_non_contiguous=True)
        k, h = cbk(WA), cbk(WH)
        iota(wv(WH), [[0, 8]], 1, 0, [h])
        sel(wv(WA), wv(WA), g8, OP.is_ge, 0.0, 0, 1, [k], [k])
        sel(wv(WH), wv(WH), g8, OP.is_ge, 64.0, 0, 1, [h], [h])
        iota(T.Mx[:, 768:784], [[0, 16]], 0, 0, ["Mx:24"])
        sel(wv(WH), wv(WH), g8, OP.is_ge, 0.0, 16, 1, [h], [h])
        sel(wv(WA), wv(WA), [[16, 8]], OP.is_ge, 0.0, 15, -1, [k], [k])
        sel(wv(WH), wv(WH), [[16, 8]], OP.is_ge, 0.0, 15, -1, [h], [h])
        iota(ev("hF"), [[0, W]], 0, 0, ["hF0"])
        sel(T.cb[:, WH + 16:WH + 17], T.cb[:, WH + 16:WH + 17], [[0, 1]], OP.is_ge, 64.0, 111, -1, [h], [h])
        iota(ev("tF"), [[0, W]], 0, 0, ["tF0"])

    def consts_step(k):
        if k < 6:
            sa(T.Pb[:, 256 * k:256 * k + 256], T.Iw[:, 256 * k:256 * k + 256], AF.Identity, Iwk, ck("Pb", 256 * k, 256 * k + 256))
        if k == 6:
            sa(T.cf[:, IS:IS + W], T.cf[:, IF:IF + W], AF.Identity, [cfk(IF)], [cfk(IS)], scale=1.0 / LQ)
            sa(T.cf[:, NI:NI + W], T.cf[:, IF:IF + W], AF.Identity, [cfk(IF)], [cfk(NI)], scale=-1.0)
        if k == 7:
            sa(T.cb[:, IB:IB + W], T.cf[:, IF:IF + W], AF.Identity, [cfk(IF)], [cbk(IB)])
            sa(T.vW[:, :], T.vW[:, :], AF.Identity, ["vW", "c9"], ["vW"], bias=col(9))

    def after(k, X, j):
        a, m, b = OPT["chunks"][j]
        if k == 9:
            m = m // 64 * 64
            sa(T.X9[:, m // 64:b // 64], T[X][:, m:b], AF.Identity, ck(X, m, b), ck("X9", m, b))
            sel(T.X9[:, a // 64:m // 64], T[X][:, a:m], [[0, m - a]], OP.is_ge, 0.0, 0, 0, ck(X, a, m), ck("X9", a, m))
            wrapv("p%d" % j, 0, (b - a) // 16, WC, lambda i: T.X9[:, a // 64:b // 64, i // 4:16:4, i % 4], ck("X9", a, b))
        else:
            xb = "Xb0" if k == 0 else "Xb"
            sa(T[xb][:, m:b], T[X][:, m:b], AF.Identity, ck(X, m, b), ck(xb, m, b))
            sel(T[xb][:, a:m], T[X][:, a:m], [[0, m - a]], OP.is_ge, 0.0, 0, 0, ck(X, a, m), ck(xb, a, m))
            wrap("p%d" % j, 0, WC, xb, a, b)
        sa(T.Y[:, a:b], T[X][:, a:b], AF.Identity, ck(X, a, b) + ["c4", "yb"], ck("Y", a, b), bias=T.yb[:, k:k + 1], scale=col(4))

    def static(c, src, b):
        bank, a = "p%d" % (5 + b), 512 * b
        mm([(T[bank][:, :], T.cb[:, c:c + 128], T[src][:, a:a + 512], c == MU, c == MP)], [cbk(c)] + ck(src, a, a + 512), bank)

    def lcopy(j):
        a, m, b = OPT["chunks"][j]
        cp(T.Lc[:, a // 16:b // 16], T["p%d" % j][:, 0:(b - a) // 16], ["#p%d" % j], ["Lc%d" % j])

    ev = lambda name: T[name][:, 0:2 * W:2]
    od = lambda name: T[name][:, 1:2 * W:2]

    def pick(out, flag, data, rd):
        op("v", lambda: vec.tensor_tensor_scan(T[out][:, :], T[flag][:, :], T[data][:, :], 0.0, OP.mult, OP.add), [flag] + rd, [out])

    def pieces(k, j):
        a, m, b = OPT["chunks"][j]
        return ((a, m), (m, b)) if OPT["split"] else ((a, b),)

    for rnd in range(2):
        tl, ul, fl, tW, tN = "tl%d" % rnd, "ul%d" % rnd, "fl%d" % rnd, "tW%d" % rnd, "tW%d" % (rnd + 1)
        cuts = OPT["scatter"]
        cp(T.Tt[:, 0:cuts[1]], T.Iw[:, :].indirect(T[tl][:, 0:cuts[1] // 16]), Iwk + [tl], ck("Tt", 0, cuts[1]))
        for a, b in zip(cuts[1:], cuts[2:]):
            sa(T.Tt[:, a:b], T.Iw[:, :].indirect(T[tl][:, a // 16:b // 16]), AF.Identity, Iwk + [tl], ck("Tt", a, b))
        if rnd == 0:
            ts(col(9), pm, float(W), None, OP.mult, None, ["pm"], ["c9"])
        for a, b in zip(cuts, cuts[1:]):
            tt(T.Al[:, :].indirect(T[ul][:, a // 16:b // 16]), T.Tt[:, a:b], T.Ic[:, a:b], OP.add, ck("Tt", a, b) + Ick + [ul], ck("Al"))
        if rnd == 0:
            consts_early()
            dma("y", [(T.Z[:, V * j:V * j + V], T.xin[:, :]) for j in range(3)] + [(T.Z[:, 3 * V:ZW], T.xin[:, 0:ZW - 3 * V])],
                "zz", ck("xin") + ["Al:0"], ck("Z", 0, ZW))
            for k in range(NSTEP):
                sa(T.yb[:, k:k + 1], col(4), AF.Identity, ["c4"], ["yb%d" % k], bias=BIG, scale=-BIG - 2.0 ** k)
            mark((SEM["s"], cnt[SEM["s"]]), "s", [], ["yb"])
        sa(T.Ub[:, :], T.Iw[:, :].indirect(T[ul][:, :]), AF.Identity, Iwk + [ul], ck("Ub"))
        for b in range(3):
            static(MU, "Ub", b)
        wrap("p3", W, WU, "Ub")
        gather2("Be", "Al", V, fl, 768)
        chunks, copies = OPT["chunks"], OPT["copies"]
        for j, (a, m, b) in enumerate(chunks):
            if j == 0:
                gather2("X0", "Be", V, ul, OPT["x0"], a, b)
            for e, (c, d) in enumerate(pieces(0, j)):
                if j > 0:
                    gv("X0", "Be", V, ul, c, d)
                if d == b:
                    after(0, "X0", j)
                for i in copies.get((j, e), ()):
                    if i <= j:
                        lcopy(i)
        for k in range(NSTEP - 1):
            X, Xn = ("X0", "X1") if k % 2 == 0 else ("X1", "X0")
            for j, (a, m, b) in enumerate(chunks):
                for e, (c, d) in enumerate(pieces(k + 1, j)):
                    tt(T[Xn][:, c:d], T[X][:, :].indirect(T.Lc[:, c // 16:d // 16]), T.Y[:, c:d], OP.min,
                       ck(X) + ["Lc%d" % j] + ck("Y", c, d), ck(Xn, c, d))
                    if k < 9 and d == b:
                        after(k + 1, Xn, j)
                        if j == 0 and 1 <= k <= 4:
                            mm([(T.p3[:, 0:W], T.cb[:, WS + 16 - i:WS + 144 - i], T.Xb0[:, i:V:16], i == 0, i == 15)
                                for i in range(4 * k - 4, 4 * k)], ck("Xb0") + [cbk(WS)], "p3")
                    for i in copies.get((j, e), ()):
                        if k < 9 or i > j:
                            lcopy(i)
            if k == 9:
                for q in range(4):
                    cp(T.Ld[:, 24 * q:24 * q + 24], T.p4[:, q:W:4], ["#p4"], ["Ld%d" % q])
            if rnd == 0:
                consts_step(k)
            if 1 <= k <= 6:
                static(MS if k % 2 else MP, "Xb0" if k % 2 else "Pb", (k - 1) // 2)
            if k == 8:
                if rnd == 0:
                    consts_late()
                wrapv("p4", 0, W, WC, lambda i: T.X9[:, :, i, :], ck("X9"))
                for q in range(4):
                    sa(T.Tt[:, 384 * q:384 * q + 384], T.X1[:, q:V:4], AF.Identity, ck("X1") + ["c4", "yb"], ck("Tt", 384 * q, 384 * q + 384),
                       bias=T.yb[:, 10:11], scale=col(4))
                for b in range(3):
                    bank, a = "p%d" % (5 + b), 512 * b
                    sa(T.St[:, a:a + 512], T[bank][:, :], AF.Identity, ["#" + bank], ck("St", a, a + 512))
                mm([(P("p0", 0), T.cf[0:2, KA:KA + W], T.cf[0:2, KB:KB + 128], True, False)], [cfk(KA), cfk(KB)], "p0")
                sa(T.sW[:, :], T.p3[:, 0:W], AF.Identity, ["#p3"], ["sW"])
                sa(od("hD"), T.p3[:, W:2 * W], AF.Identity, ["#p3"], ["uW"])
        for q in range(4):
            a, b = 384 * q, 384 * q + 384
            tt(T.Be[:, a:b], T.X0[:, :].indirect(T.Ld[:, 24 * q:24 * q + 24]), T.Tt[:, a:b], OP.min,
               ck("X0") + ["Ld%d" % q] + ck("Tt", a, b), ck("Be", a, b))
            mm([(T.p0[0:W, 4 * j + q:128:16], T.Be[:, a + j:b:4], T.cf[:, SK:SK + 8], False, q == 3 and j == 3) for j in range(4)],
               ck("Be", a, b) + [cfk(SK)], "p0")
        if rnd == 0:
            cp(T.tW0[:], T.ti[:], ["ti"], ["tW0"])
        tt(T.w2[:, :], T.sW[:, :], T[tW][:, :], OP.subtract, ["sW", tW], ["w2"])
        D0 = P("p0", 0)
        ts(Eb, D0, 0.0, None, OP.max, None, ["#p0"], ["E"])
        ts(U("oi"), D0, 0.0, None, OP.max, None, ["#p0"], ["oi"])
        op("v", lambda: vec.tensor_tensor_scan(U("Sc"), U("rst"), Eb, 0.0, OP.mult, OP.add), ["rst", "E"], ["Sc"])
        mm([(P("p4", 0), T.cf[0:W, TR:TR + W], Eb, True, False)], [cfk(TR), "E"], "p4")
        mm([(P("p4", 0), T.cf[0:W, ON:ON + W], U("Sc"), False, True)], [cfk(ON), "Sc"], "p4")
        sa(Dr(RO), Eb, AF.Identity, ["E"], Dk(RO))
        ts(U("pr"), U("oi"), 1, None, OP.bitwise_and, None, ["oi"], ["pr"])
        ts(U("rD"), D0, M1 * LQ, -M1 * LQ, OP.add, OP.add, ["#p0"], ["rD"])
        ts(U("gg"), U("pr"), 1.0 + 2.0 ** -13, None, OP.add, None, ["pr"], ["gg"])
        flip("p1", 0, [("rD", IS)], "vW")
        tt(Dr(RO + 1), D0, Dr(RO), OP.subtract, ["#p0"] + Dk(RO), Dk(RO + 1))
        sa(Dr(RD), U("gg"), AF.Identity, ["gg"], Dk(RD), bias=-1.0 - 2.0 ** -13)
        tt(U("zz"), P("p4", 0), U("gg"), OP.mult, ["#p4", "gg"], ["zz"])
        tt(U("dd"), D0, U("rD"), OP.subtract, ["#p0", "rD"], ["dd"])
        ts(P("p4", 1), U("zz"), 2 * M1, -2 * M1, OP.add, OP.add, ["zz"], ["#p4"])
        sa(Dr(RA), U("zz"), AF.Identity, ["zz"], Dk(RA))
        cp(T.Ll[:, :], T.p1[:, 0:W], ["#p1"], ["Ll"])
        tt(Dr(RA + 1), P("p4", 1), Dr(RA), OP.subtract, ["#p4"] + Dk(RA), Dk(RA + 1))
        sa(U("q2"), U("dd"), AF.Identity, ["dd"], ["q2"], bias=-1.0, scale=2.0)
        sa(U("QE"), U("dd"), AF.Identity, ["dd"], ["QE"], bias=1.0, scale=-2.0)
        for b, bank in enumerate(("p5", "p6", "p7", "p2")):
            mm([(T[bank][:, W * j:W * j + W], T.D[0:W, :, :, 4 * b + j], T.cb[0:W, IB:IB + W], True, True) for j in range(4)],
               Dk(*range(16)) + [cbk(IB)], bank)
            if b % 2 == 0:
                sa(T.R[:, 384 * b:384 * b + 384], T[bank][:, 0:384], AF.Identity, ["#" + bank], ck("R", 384 * b, 384 * b + 384))
            else:
                cp(T.R[:, 384 * b:384 * b + 384], T[bank][:, 0:384], ["#" + bank], ck("R", 384 * b, 384 * b + 384))
        mm([(T.p1[0:W, 0:256], T.cf[0:W, IF:IF + W], T.QE[0:W, :], True, False)], [cfk(IF), "QE", "E"], "p1")
        gather2("Gl", "R", V, "Ll", 768)
        turn("p4", 24, T.cb[:, SA:SA + 24], ["sa0", "sa1", "sa2"], "Gl")
        tt(U("bb"), P("p4", 0), U("q2"), OP.is_le, ["#p4", "q2"], ["bb"])
        tt(U("Aq"), P("p4", 2), U("q2"), OP.add, ["#p4", "q2"], ["Aq"])
        mm([(T.p2[:, 0:W], U("Aq"), T.cf[0:W, IF:IF + W], True, False)], ["Aq", cfk(IF)], "p2")
        tt(U("mm"), P("p4", 1), U("bb"), OP.mult, ["#p4", "bb"], ["mm"])
        mm([(T.p2[:, 0:W], U("mm"), T.cf[0:W, IF:IF + W], False, True)], ["mm", cfk(IF)], "p2")
        turn("p1", 16, T.cb[:, SB:SB + 16], ["sb0", "sb1"], "Gl", True)
        sa(U("sg"), P("p1", 0), AF.Sign, ["#p1"], ["sg"], bias=-0.5)
        sa(U("oo"), P("p1", 1), AF.Relu, ["#p1"], ["oo"], bias=-4096.0)
        cp(T.Lp[:, :], T.p2[:, 0:W], ["#p2"], ["Lp"])
        tt(T.Z[:, :].indirect(T.Lp[:, :]), T.Gl[:, :], T.St[:, :], OP.add, ck("Gl") + ck("St") + ["Lp"], ck("Z", 0, ZW))
        sa(T.Gs[:, :], T.Gl[:, :].indirect(T[tl][:, :]), AF.Identity, ck("Gl") + [tl], ck("Gs"))
        flip("p3", 0, [("Aq", IF), ("mm", IF), ("sg", IF), ("oo", NI)])
        wrap("p4", 0, WL, "Gl")
        for bank, a, b in (("p6", 0, 512), ("p7", 512, 768)):
            mm([(T[bank][:, 0:b - a], T.cb[:, FP:FP + 128], T.Pb[:, a:b], True, False)], ck("Pb") + [cbk(FP)], bank)
        wrap("p5", 0, WL, "Gs")
        sa(T.nW[:, :], T.p4[:, 0:W], AF.Sign, ["#p4"], ["nW"], bias=768.0, scale=-1.0)
        sa(T.p4[:, W:2 * W], T.nW[:, :], AF.Relu, ["nW"], ["#p4"])
        wrap("p0", 0, WP, "Z", 0, V, 32, 0)
        wrap("p1", 0, WP, "Z", 0, V, 32, 1)
        for bank, a, b in (("p6", 0, 512), ("p7", 512, 768)):
            mm([(T[bank][:, 0:b - a], T.cb[:, FA:FA + 128], T.Z[:, 2 * a:2 * b:2], False, True)], ck("Z") + [cbk(FA)], bank)
        cp(T.Lq[:, :], T.p3[:, 0:W], ["#p3"], ["Lq"])
        ts(T.Le[:, :], T.p4[:, 0:W], 768.0, None, OP.min, None, ["#p4"], ["Le"])
        h0, h1, h2, h3 = OPT["half"]
        gs("Gh", "Z", ZW, "Lq", 0, h0)
        gv("Gh", "Z", ZW, "Lq", h0, h1)
        cp(T.Lo[:, 0:48], T.p0[:, 0:48], ["#p0"], ["Lo0"])
        gv("Gh", "Z", ZW, "Lq", h1, h2)
        cp(T.Lo[:, 48:96], T.p1[:, 0:48], ["#p1"], ["Lo1"])
        gv("Gh", "Z", ZW, "Lq", h2, h3)

        def low(a, b):
            sa(T.xlo[:, a:b], T.xin[:, :].indirect(T.Lo[:, a // 16:b // 16]), AF.Identity, ck("xin") + ["Lo0"], ck("xlo", a, b))

        def gap(a, b):
            tt(T.df[:, a:b], T.xin[:, :].indirect(T.Lo[:, 48 + a // 16:48 + b // 16]), T.xlo[:, a:b], OP.subtract,
               ck("xin") + ["Lo1"] + ck("xlo", a, b), ck("df", a, b))

        def size(a, b):
            sa(T.ad[:, a:b], T.df[:, a:b], AF.Abs, ck("df", a, b), ck("ad", a, b))

        def scan(a, b):
            bank = "p%d" % (6 + a // 512)
            init = 0.0 if a == 0 else T.Mx[:, a - 1:a]
            op("v", lambda: vec.tensor_tensor_scan(T.Mx[:, a:b], T[bank][:, a % 512:a % 512 + b - a], T.ad[:, a:b], init, OP.min, OP.max),
               ["#" + bank] + ck("ad", a, b) + ck("Mx", 0, a), ck("Mx", a, b))

        def agree_v(out, lst, a, b):
            ts(T[out][:, a:b], T.Mx[:, :].indirect(T[lst][:, a // 16:b // 16]), T.thf[:, 0:1], 0.5, OP.is_le, OP.subtract,
               ck("Mx", 0, 784) + [lst, "thf"], ck(out, a, b))

        def agree_s(out, lst, a, b):
            sa(T[out][:, a:b], T.Mx[:, :].indirect(T[lst][:, a // 16:b // 16]), AF.Sign, ck("Mx", 0, 784) + [lst, "thb"], ck(out, a, b),
               bias=T.thb[:, 0:1], scale=-1.0)

        c0, c1, c2 = OPT["pairs"]
        low(*c0)
        low(*c1)
        low(*c2)
        gs("Gh", "Z", ZW, "Lq", h3, V)
        wrap("p2", 0, WU, "Gh")
        wrap("p3", 0, WS, "Gh")
        gap(*c0)
        gap(*c1)
        size(*c0)
        gap(*c2)
        size(*c1)
        size(*c2)
        if rnd == 0:
            cp(T.thf[:, 0:1], T.thi[:, 0:1], ["thi"], ["thf"])
            sa(T.thb[:, 0:1], T.thf[:, 0:1], AF.Identity, ["thf"], ["thb"], bias=0.5)
        ts(T.Lf[:, :], T.p5[:, 0:W], 768.0, None, OP.min, None, ["#p5"], ["Lf"])
        scan(c0[0], c1[1])
        tt(T.w3[:, :], T.p4[:, W:2 * W], T.w2[:, :], OP.mult, ["#p4", "w2"], ["w3"])
        tt(ev("hD"), T.p2[:, 0:W], od("hD"), OP.subtract, ["#p2", "uW"], ["w4"])
        scan(*c2)
        tt(od("tD"), T.w3[:, :], T[tW][:, :], OP.add, ["w3", tW], ["w7"])
        agree_v("Ga", "Le", 0, 768)
        agree_s("Ga", "Le", 768, V)
        wrap("p0", 0, WH, "Ga")
        agree_s("Gb", "Lf", OPT["mirror"], V)
        agree_v("Gb", "Lf", 0, OPT["mirror"])
        wrap("p1", 0, WA, "Gb")
        ts(od("hF"), T.p0[:, 0:W], -32.0, None, OP.is_ge, None, ["#p0", "hF0"], ["hF"])
        ts(T.w5[:, :], T.p0[:, 0:W], 64 * M1, -64 * M1, OP.add, OP.add, ["#p0"], ["w5"])
        tt(ev("tD"), T.p3[:, 0:W], od("tD"), OP.subtract, ["#p3", "w7"], ["w1"])
        pick("hO", "hF", "hD", ["w4", "uW"])
        tt(T.w8[:, :], T.p0[:, 0:W], T.w5[:, :], OP.is_ge, ["#p0", "w5"], ["w8"])
        hs = "hs" if rnd == 0 else "hf"
        cp(T[hs][:, :], od("hO"), ["hO"], [hs])
        send(T[hs][:], hs, 1 + 2 * rnd)
        ts(T.p1[:, W:2 * W], T.p1[:, 0:W], 0.0, None, OP.is_ge, None, ["#p1"], ["#p1"])
        tt(od("tF"), T.p1[:, W:2 * W], T.w8[:, :], OP.not_equal, ["#p1", "w8", "tF0"], ["tF"])
        pick("tO", "tF", "tD", ["w1", "w7"])
        if rnd == 0:
            cp(T.tl1[:, :], od("tO"), ["tO"], ["tl1"])
            send(T.tl1[:], "tl1", 2)
            sa(T[tN][:, :], od("tO"), AF.Identity, ["tO"], [tN])
        else:
            cp(T[tN][:, :], od("tO"), ["tO"], [tN])
    dma("y", [(T.yt[:], T.tW2[:])], "st0", ["tW2"], [])
    dma("s", [(T.yu[:], T.yl[:])], "st1", ["yl"], [])
    for s, c in cnt.items():
        if clock["g"].get(s, 0) < c:
            g.wait_ge(T.sem[s], c)
